import numpy as np
import ml_dtypes


def mxq(x, axis, fmt="e4m3"):
    dtype, down = {"e4m3": (ml_dtypes.float8_e4m3fn, 7), "e5m2": (ml_dtypes.float8_e5m2, 14)}[fmt]
    v = np.moveaxis(np.asarray(x, np.float32).astype(ml_dtypes.bfloat16).astype(np.float64), axis, -1)
    blocks = v.reshape(v.shape[:-1] + (-1, 32))
    amax = np.abs(blocks).max(-1, keepdims=True)
    byte = np.maximum(np.where(amax > 0, np.frexp(amax)[1] - 1 + 127, 0) - down, 1)
    scale = np.exp2(byte - 127.0)
    codes = (blocks / scale).astype(np.float32).astype(dtype).astype(np.float64)
    return np.moveaxis((codes * scale).reshape(v.shape), -1, axis)


WIDE = False


def mx_kscale(k):
    if not WIDE:
        return np.ones(k)
    levels = np.array([10, -10, 5, -5, 0])
    if k % 512:
        return np.exp2(np.random.permutation(np.resize(levels, k // 32))).repeat(32)
    a = np.empty((k // 512, 16))
    for p in range(k // 512):
        a[p, :8] = np.random.permutation(np.resize(levels, 8))
        for g in range(8):
            far = levels[np.abs(levels - a[p, g]) >= 10]
            a[p, g + 8] = far[np.random.randint(len(far))]
    return np.exp2(a.ravel()).repeat(32)


def f64(x):
    return np.asarray(x).astype(np.float64)


def striped(idx):
    return np.tile(idx.reshape(-1, 16).T, (8, 1)).astype(np.uint16)


def unstriped(offs):
    return offs[:16].T.reshape(-1).astype(np.int64)


E2M1 = np.array([0.0, 0.5, 1.0, 1.5, 2.0, 3.0, 4.0, 6.0, -0.0, -0.5, -1.0, -1.5, -2.0, -3.0, -4.0, -6.0])


def pack_weight(w, fmt):
    k, n = w.shape
    w = f64(np.asarray(w, np.float32).astype(ml_dtypes.bfloat16)).reshape(k // 32, 32, n)
    amax = np.abs(w).max(1)
    if fmt == "e4m3":
        byte = np.frexp(amax)[1] - 1 + 127 - 7
    else:
        mant, ex = np.frexp(amax / 6.0)
        byte = np.where(mant > 0.5, ex, ex - 1) + 127
    byte = np.clip(np.where(amax > 0, byte, 1), 1, 254)
    scaled = (w * np.exp2(127.0 - byte)[:, None, :]).reshape(k, n).astype(np.float32)
    by_word = np.ascontiguousarray(scaled.reshape(k // 512, 128, 4, n).transpose(0, 1, 3, 2))
    if fmt == "e4m3":
        words = by_word.astype(ml_dtypes.float8_e4m3fn).view(np.uint8)
    else:
        c = by_word.astype(ml_dtypes.float4_e2m1fn).view(np.uint8) & 0xF
        words = (c[..., 0::2] | (c[..., 1::2] << 4)).reshape(k // 512, 128, 2 * n)
    return np.ascontiguousarray(words), np.ascontiguousarray(byte.astype(np.uint8).reshape(k // 512, 16, n))


def unpack_weight(words, scales, fmt):
    g, _, n = scales.shape
    words = np.ascontiguousarray(words).reshape(g, 128, n, -1)
    if fmt == "e4m3":
        vals = words.view(ml_dtypes.float8_e4m3fn).astype(np.float64)
    else:
        nib = np.empty((g, 128, n, 4), np.uint8)
        nib[..., 0::2] = words & 0xF
        nib[..., 1::2] = words >> 4
        vals = E2M1[nib]
    vals = vals * np.repeat(np.exp2(scales.astype(np.float64) - 127.0), 8, axis=1)[..., None]
    return vals.transpose(0, 1, 3, 2).reshape(g * 512, n)


def gelu(v):
    return 0.5 * v * (1.0 + np.tanh(np.sqrt(2.0 / np.pi) * (v + 0.044715 * v**3)))


K, H, N, T, S = 512, 1024, 256, 4096, 1024

def setup_inputs():
    n = np.random.standard_normal
    s = mx_kscale(K)[:, None]
    u = mx_kscale(H)[:, None]
    tab_words, tab_scales = pack_weight(n((K, T)) * s, "e4m3")
    tab2_words, tab2_scales = pack_weight(n((K, T)) * s, "e4m3")
    w4_words, w4_scales = pack_weight(n((H, N)) / np.sqrt(H) / u, "e2m1")
    return {
        "tab_words": tab_words, "tab_scales": tab_scales,
        "tab2_words": tab2_words, "tab2_scales": tab2_scales,
        "offs": striped(np.random.permutation(T)[:S]),
        "offs2": striped(np.random.permutation(T)[:S]),
        "w1": (n((K, H)) / np.sqrt(K) / s).astype(np.float32),
        "gain": (np.exp(0.3 * n(H)) * u[:, 0]).astype(np.float32),
        "w4_words": w4_words, "w4_scales": w4_scales,
        "bias": (0.5 * n(N)).astype(np.float32),
    }

def reference(tab_words, tab_scales, tab2_words, tab2_scales, offs, offs2, w1, gain, w4_words, w4_scales, bias):
    v = unpack_weight(tab_words, tab_scales, "e4m3")[:, unstriped(offs)]
    v2 = unpack_weight(tab2_words, tab2_scales, "e4m3")[:, unstriped(offs2)]
    w4 = unpack_weight(w4_words, w4_scales, "e2m1")
    w1q = mxq(f64(w1), 0, "e4m3")
    a = np.tanh(w1q.T @ v)
    b = np.tanh(w1q.T @ v2)
    h = f64(gain)[:, None] * (b - a)
    hq = mxq(h, 0, "e4m3")
    return (w4.T @ hq) + f64(bias)[:, None]

@@ -1,0 +1,236 @@
+from contextlib import ExitStack
+
+import concourse.mybir as mybir
+from concourse.masks import make_identity
+
+K, H, N, T, S = 512, 1024, 256, 4096, 1024
+FLOPS = 2 * K * H * S * 2 + 2 * H * N * S
+
+F32 = mybir.dt.float32
+BF16 = mybir.dt.bfloat16
+I32 = mybir.dt.int32
+U32 = mybir.dt.uint32
+U16 = mybir.dt.uint16
+U8 = mybir.dt.uint8
+FP8X4 = mybir.dt.float8_e4m3fn_x4
+FP4X4 = mybir.dt.float4_e2m1fn_x4
+ACT = mybir.ActivationFunctionType
+ALU = mybir.AluOpType
+
+P = 128
+PACK = 4
+PASS = P * PACK
+HALF = 512
+TILES = HALF // P
+
+
+def tile_list_replay_inverse_dynamics_kernel(
+    tc, tab_words, tab_scales, tab2_words, tab2_scales, offs, offs2, w1, gain, w4_words, w4_scales, bias, out
+):
+    nc = tc.nc
+    with ExitStack() as ctx:
+        keep = ctx.enter_context(tc.tile_pool(name="keep", bufs=1))
+        zps = ctx.enter_context(tc.psum_pool(name="zps", bufs=3))
+        dps = ctx.enter_context(tc.psum_pool(name="dps", bufs=3))
+        ops = ctx.enter_context(tc.psum_pool(name="ops", bufs=2))
+
+        def held(name, shape, dtype):
+            return keep.tile(shape, dtype, name=name, align_bytes=64)
+
+        lists = [keep.tile([P, S // 16], U16, name=f"list{i}") for i in range(2)]
+        words = [held(f"words{i}", [P, T], I32) for i in range(2)]
+        planes = [held(f"planes{i}", [P, T // 4], I32) for i in range(2)]
+        w1_raw = [held(f"w1raw{b}", [P, PACK, PASS], F32) for b in range(2)]
+        w4_codes = held("w4codes", [P, 2, 2 * N // 4], I32)
+        w4_plane = held("w4plane", [P, 2, N // 4], I32)
+        gains = held("gains", [P, 2, PACK], F32)
+        biases = held("biases", [P, 2], F32)
+        ident = held("ident", [P, P], F32)
+        warm = held("warm", [P, 8], F32)
+
+        nc.vector.memset(planes[0][:], 0)
+        nc.gpsimd.memset(planes[1][:], 0)
+        nc.vector.memset(warm[:, 0:4], 0.0)
+        nc.vector.memset(w4_plane[:], 0)
+        nc.scalar.activation(warm[:, 4:8], warm[:, 0:4], ACT.Tanh)
+
+        def load_words(i, src):
+            nc.sync.dma_start(words[i][:], src[0].rearrange("p t i -> p (t i)").bitcast(I32))
+
+        def load_plane(i, src):
+            for r in range(4):
+                nc.sync.dma_start(planes[i][4 * i + r : P : 32, :], src[0].bitcast(I32)[r:16:4, :])
+
+        w1_rows = w1.rearrange("(p i) c -> p i c", i=PACK)
+        nc.sync.dma_start(lists[0][:], offs)
+        nc.sync.dma_start(w1_raw[0][:], w1_rows[:, :, 0:PASS])
+        load_plane(0, tab_scales)
+        load_words(0, tab_words)
+        nc.sync.dma_start(lists[1][:], offs2)
+        load_plane(1, tab2_scales)
+        nc.sync.dma_start(gains[:], gain.rearrange("(b p t) -> p b t", b=2, t=PACK))
+        nc.sync.dma_start(w1_raw[1][:], w1_rows[:, :, PASS : 2 * PASS])
+        load_words(1, tab2_words)
+        with nc.allow_non_contiguous_dma(reason="one bias for each partition"):
+            nc.sync.dma_start(biases[:], bias.rearrange("(c p) -> p c", p=P))
+        nc.sync.dma_start(w4_codes[:], w4_words.bitcast(I32).rearrange("a p c -> p a c"))
+        for r in range(4):
+            nc.sync.dma_start(
+                w4_plane[r:P:32, :, :], w4_scales.bitcast(I32)[:, r:16:4, :].rearrange("a q c -> q a c")
+            )
+        make_identity(nc, ident[:])
+
+        w1_bf = [held(f"w1bf{b}", [P, PASS, PACK], BF16) for b in range(2)]
+        w1_codes = [held(f"w1codes{b}", [P, PASS], U32) for b in range(2)]
+        w1_plane = [held(f"w1plane{b}", [P, PASS], U8) for b in range(2)]
+        picked_words = [[held(f"pw{i}{h}", [P, HALF], U32) for h in range(2)] for i in range(2)]
+        picked_plane = [[held(f"pp{i}{h}", [P, HALF], U8) for h in range(2)] for i in range(2)]
+
+        def gather_words(i, h):
+            offsets = lists[i][:, 32 * h : 32 * (h + 1)]
+            nc.vector.tensor_copy(picked_words[i][h][:], words[i][:].bitcast(U32).indirect(offsets))
+
+        def gather_plane(i, h):
+            offsets = lists[i][:, 32 * h : 32 * (h + 1)]
+            nc.vector.tensor_copy(picked_plane[i][h][:], planes[i][:].bitcast(U8).indirect(offsets))
+
+        def quantize(codes, plane, src):
+            nc.vector.quantize_mx(out=codes.bitcast(FP8X4), scales=plane, in_=src.rearrange("p c i -> p (c i)"))
+
+        nc.scalar.activation(
+            w1_bf[0][:].rearrange("p (t m) i -> p m i t", t=PACK),
+            w1_raw[0][:].rearrange("p i (m t) -> p m i t", t=PACK),
+            ACT.Copy,
+        )
+
+        enc0 = [[[held(f"enc0_{i}{h}{t}", [P, HALF], F32) for t in range(PACK)] for h in range(2)] for i in range(2)]
+        enc1 = [[held(f"enc1_{i}{j}", [P, PACK, P], F32) for j in range(S // P)] for i in range(2)]
+
+        def encode0(i, h):
+            for t in range(PACK):
+                z = zps.tile([P, HALF], F32, name="z")
+                cols = slice(P * t, P * (t + 1))
+                nc.tensor.matmul_mx(
+                    out=z[:],
+                    lhsT=w1_codes[0][:, cols].bitcast(FP8X4),
+                    lhsT_scale=w1_plane[0][:, cols],
+                    rhs=picked_words[i][h][:].bitcast(FP8X4),
+                    rhs_scale=picked_plane[i][h][4 * i : P, :],
+                    start=True,
+                    stop=True,
+                )
+                nc.scalar.activation(enc0[i][h][t][:], z[:], ACT.Tanh)
+
+        def encode1(i, j):
+            h, cols = j // TILES, slice(P * (j % TILES), P * (j % TILES + 1))
+            z = zps.tile([P, PASS], F32, name="z")
+            nc.tensor.matmul_mx(
+                out=z[:],
+                lhsT=picked_words[i][h][:, cols].bitcast(FP8X4),
+                lhsT_scale=picked_plane[i][h][4 * i : P, cols],
+                rhs=w1_codes[1][:].bitcast(FP8X4),
+                rhs_scale=w1_plane[1][:],
+                start=True,
+                stop=True,
+            )
+            nc.scalar.activation(
+                enc1[i][j][:], z[:].rearrange("p (m t) -> p t m", t=PACK), ACT.Tanh, scale=(-1.0 if i == 0 else 1.0)
+            )
+
+        gather_words(0, 0)
+        gather_plane(0, 0)
+        quantize(w1_codes[0][:], w1_plane[0][:], w1_bf[0][:])
+        encode0(0, 0)
+        gather_words(0, 1)
+        gather_plane(0, 1)
+        encode0(0, 1)
+        nc.vector.tensor_copy(
+            w1_bf[1][:].rearrange("p (c e) i -> p c i e", e=4), w1_raw[1][:].rearrange("p i (c e) -> p c i e", e=4)
+        )
+        gather_words(1, 0)
+        gather_plane(1, 0)
+        quantize(w1_codes[1][:], w1_plane[1][:], w1_bf[1][:])
+        for j in range(TILES):
+            encode1(0, j)
+        gather_words(1, 1)
+        gather_plane(1, 1)
+
+        scaled = [[held(f"scaled{h}{t}", [P, HALF], F32) for t in range(PACK)] for h in range(2)]
+        for h in range(2):
+            for t in range(PACK):
+                nc.vector.tensor_scalar(scaled[h][t][:], enc0[0][h][t][:], gains[:, 0, t : t + 1], None, ALU.mult)
+
+        h_rows = [held(f"hrows{h}", [P, PACK, HALF], BF16) for h in range(2)]
+        h_bf0 = [held(f"hbf0{h}", [P, HALF, PACK], BF16) for h in range(2)]
+        h_bf1 = [held(f"hbf1{h}", [P, HALF, PACK], BF16) for h in range(2)]
+        h_codes = [[held(f"hcodes{a}{h}", [P, HALF], U32) for h in range(2)] for a in range(2)]
+        h_plane = [[held(f"hplane{a}{h}", [P, HALF], U8) for h in range(2)] for a in range(2)]
+        gain1 = gains[:, 1:2, :].to_broadcast([P, P, PACK])
+
+        def change0(h):
+            for t in range(PACK):
+                nc.vector.scalar_tensor_tensor(
+                    h_rows[h][:, t, :], enc0[1][h][t][:], gains[:, 0, t : t + 1], scaled[h][t][:], ALU.mult, ALU.subtract
+                )
+
+        def interleave0(h):
+            nc.vector.tensor_copy(
+                h_bf0[h][:].rearrange("p (c e) t -> p c t e", e=4), h_rows[h][:].rearrange("p t (c e) -> p c t e", e=4)
+            )
+
+        def change1(j):
+            d = dps.tile([P, PACK, P], F32, name="d")
+            for t in range(PACK):
+                for i in range(2):
+                    nc.tensor.matmul(
+                        d[:, t, :], enc1[i][j][:, t, :], ident[:], start=(i == 0), stop=(i == 1), is_transpose=True
+                    )
+            cols = slice(P * (j % TILES), P * (j % TILES + 1))
+            nc.vector.tensor_tensor(h_bf1[j // TILES][:, cols, :], d[:].rearrange("p t j -> p j t"), gain1, ALU.mult)
+
+        out_rows = out.rearrange("(c p) j -> p c j", p=P)
+
+        def product(acc, c, h, cols):
+            for a in range(2):
+                nc.tensor.matmul_mx(
+                    out=acc,
+                    lhsT=w4_codes[:, a, 64 * c : 64 * (c + 1)].bitcast(U8).bitcast(FP4X4),
+                    lhsT_scale=w4_plane[:, a, 32 * c : 32 * (c + 1)].bitcast(U8),
+                    rhs=h_codes[a][h][:, cols].bitcast(FP8X4),
+                    rhs_scale=h_plane[a][h][:, cols],
+                    start=(a == 0),
+                    stop=(a == 1),
+                )
+
+        def logits(h, first, width):
+            cols = slice(first, first + width)
+            quantize(h_codes[1][h][:, cols], h_plane[1][h][:, cols], h_bf1[h][:, cols, :])
+            res = held(f"res{h}_{first}", [P, 2, width], F32)
+            for c in range(2):
+                acc = ops.tile([P, width], F32, name="acc")
+                step = HALF if width == HALF else P
+                for n0 in range(0, width, step):
+                    product(acc[:, n0 : n0 + step], c, h, slice(first + n0, first + n0 + step))
+                nc.scalar.activation(res[:, c, :], acc[:], ACT.Identity, bias=biases[:, c : c + 1])
+            nc.sync.dma_start(out_rows[:, :, HALF * h + first : HALF * h + first + width], res[:])
+
+        for h in range(2):
+            encode0(1, h)
+            for j in range(TILES * h, TILES * (h + 1)):
+                if h == 1:
+                    encode1(0, j)
+                encode1(1, j)
+        for h in range(2):
+            change0(h)
+            change1(TILES * h)
+            interleave0(h)
+            change1(TILES * h + 1)
+            quantize(h_codes[0][h][:], h_plane[0][h][:], h_bf0[h][:])
+            change1(TILES * h + 2)
+            if h == 1:
+                logits(1, 0, 2 * P)
+            change1(TILES * h + 3)
+            if h == 0:
+                logits(0, 0, HALF)
+        logits(1, 2 * P, P)
+        logits(1, 3 * P, P)

@@ -30,9 +30,9 @@ def tile_list_replay_inverse_dynamics_kernel(
     nc = tc.nc
     with ExitStack() as ctx:
         keep = ctx.enter_context(tc.tile_pool(name="keep", bufs=1))
-        zps = ctx.enter_context(tc.psum_pool(name="zps", bufs=3))
-        dps = ctx.enter_context(tc.psum_pool(name="dps", bufs=3))
-        ops = ctx.enter_context(tc.psum_pool(name="ops", bufs=2))
+        ring = ctx.enter_context(tc.tile_pool(name="ring", bufs=5))
+        zps = ctx.enter_context(tc.psum_pool(name="zps", bufs=4))
+        dps = ctx.enter_context(tc.psum_pool(name="dps", bufs=4))
 
         def held(name, shape, dtype):
             return keep.tile(shape, dtype, name=name, align_bytes=64)
@@ -52,22 +52,22 @@ def tile_list_replay_inverse_dynamics_kernel(
         nc.gpsimd.memset(planes[1][:], 0)
         nc.vector.memset(warm[:, 0:4], 0.0)
         nc.vector.memset(w4_plane[:], 0)
-        nc.scalar.activation(warm[:, 4:8], warm[:, 0:4], ACT.Tanh)
 
         def load_words(i, src):
             nc.sync.dma_start(words[i][:], src[0].rearrange("p t i -> p (t i)").bitcast(I32))
 
-        def load_plane(i, src):
+        def load_plane(i, src, queue):
             for r in range(4):
-                nc.sync.dma_start(planes[i][4 * i + r : P : 32, :], src[0].bitcast(I32)[r:16:4, :])
+                queue.dma_start(planes[i][4 * i + r : P : 32, :], src[0].bitcast(I32)[r:16:4, :])
 
         w1_rows = w1.rearrange("(p i) c -> p i c", i=PACK)
         nc.sync.dma_start(lists[0][:], offs)
-        nc.sync.dma_start(w1_raw[0][:], w1_rows[:, :, 0:PASS])
-        load_plane(0, tab_scales)
-        load_words(0, tab_words)
         nc.sync.dma_start(lists[1][:], offs2)
-        load_plane(1, tab2_scales)
+        nc.sync.dma_start(w1_raw[0][:], w1_rows[:, :, 0:PASS])
+        load_plane(0, tab_scales, nc.scalar)
+        nc.scalar.activation(warm[:, 4:8], warm[:, 0:4], ACT.Tanh)
+        load_plane(1, tab2_scales, nc.sync)
+        load_words(0, tab_words)
         nc.sync.dma_start(gains[:], gain.rearrange("(b p t) -> p b t", b=2, t=PACK))
         nc.sync.dma_start(w1_raw[1][:], w1_rows[:, :, PASS : 2 * PASS])
         load_words(1, tab2_words)
@@ -104,10 +104,10 @@ def tile_list_replay_inverse_dynamics_kernel(
         )
 
         enc0 = [[[held(f"enc0_{i}{h}{t}", [P, HALF], F32) for t in range(PACK)] for h in range(2)] for i in range(2)]
-        enc1 = [[held(f"enc1_{i}{j}", [P, PACK, P], F32) for j in range(S // P)] for i in range(2)]
+        enc1 = [{}, {}]
 
-        def encode0(i, h):
-            for t in range(PACK):
+        def encode0(i, h, slots=range(PACK)):
+            for t in slots:
                 z = zps.tile([P, HALF], F32, name="z")
                 cols = slice(P * t, P * (t + 1))
                 nc.tensor.matmul_mx(
@@ -123,6 +123,7 @@ def tile_list_replay_inverse_dynamics_kernel(
 
         def encode1(i, j):
             h, cols = j // TILES, slice(P * (j % TILES), P * (j % TILES + 1))
+            enc1[i][j] = ring.tile([P, PACK, P], F32, name=f"enc1_{i}")
             z = zps.tile([P, PASS], F32, name="z")
             nc.tensor.matmul_mx(
                 out=z[:],
@@ -137,28 +138,30 @@ def tile_list_replay_inverse_dynamics_kernel(
                 enc1[i][j][:], z[:].rearrange("p (m t) -> p t m", t=PACK), ACT.Tanh, scale=(-1.0 if i == 0 else 1.0)
             )
 
-        gather_words(0, 0)
-        gather_plane(0, 0)
+        scaled = [[held(f"scaled{h}{t}", [P, HALF], F32) for t in range(PACK)] for h in range(2)]
+
+        def prescale(h):
+            for t in range(PACK):
+                nc.vector.tensor_scalar(scaled[h][t][:], enc0[0][h][t][:], gains[:, 0, t : t + 1], None, ALU.mult)
+
+        for i in range(2):
+            for h in range(2):
+                gather_plane(i, h)
         quantize(w1_codes[0][:], w1_plane[0][:], w1_bf[0][:])
+        gather_words(0, 0)
         encode0(0, 0)
         gather_words(0, 1)
-        gather_plane(0, 1)
         encode0(0, 1)
         nc.vector.tensor_copy(
             w1_bf[1][:].rearrange("p (c e) i -> p c i e", e=4), w1_raw[1][:].rearrange("p i (c e) -> p c i e", e=4)
         )
-        gather_words(1, 0)
-        gather_plane(1, 0)
+        prescale(0)
         quantize(w1_codes[1][:], w1_plane[1][:], w1_bf[1][:])
-        for j in range(TILES):
+        for j in range(TILES + 1):
             encode1(0, j)
+        prescale(1)
+        gather_words(1, 0)
         gather_words(1, 1)
-        gather_plane(1, 1)
-
-        scaled = [[held(f"scaled{h}{t}", [P, HALF], F32) for t in range(PACK)] for h in range(2)]
-        for h in range(2):
-            for t in range(PACK):
-                nc.vector.tensor_scalar(scaled[h][t][:], enc0[0][h][t][:], gains[:, 0, t : t + 1], None, ALU.mult)
 
         h_rows = [held(f"hrows{h}", [P, PACK, HALF], BF16) for h in range(2)]
         h_bf0 = [held(f"hbf0{h}", [P, HALF, PACK], BF16) for h in range(2)]
@@ -179,7 +182,7 @@ def tile_list_replay_inverse_dynamics_kernel(
             )
 
         def change1(j):
-            d = dps.tile([P, PACK, P], F32, name="d")
+            d = dps.tile([P, PACK, P], F32, name="d", tag="late")
             for t in range(PACK):
                 for i in range(2):
                     nc.tensor.matmul(
@@ -207,30 +210,39 @@ def tile_list_replay_inverse_dynamics_kernel(
             quantize(h_codes[1][h][:, cols], h_plane[1][h][:, cols], h_bf1[h][:, cols, :])
             res = held(f"res{h}_{first}", [P, 2, width], F32)
             for c in range(2):
-                acc = ops.tile([P, width], F32, name="acc")
+                acc = dps.tile([P, width], F32, name="acc", tag="late")
                 step = HALF if width == HALF else P
                 for n0 in range(0, width, step):
                     product(acc[:, n0 : n0 + step], c, h, slice(first + n0, first + n0 + step))
                 nc.scalar.activation(res[:, c, :], acc[:], ACT.Identity, bias=biases[:, c : c + 1])
             nc.sync.dma_start(out_rows[:, :, HALF * h + first : HALF * h + first + width], res[:])
 
-        for h in range(2):
-            encode0(1, h)
-            for j in range(TILES * h, TILES * (h + 1)):
-                if h == 1:
-                    encode1(0, j)
-                encode1(1, j)
-        for h in range(2):
-            change0(h)
-            change1(TILES * h)
-            interleave0(h)
-            change1(TILES * h + 1)
-            quantize(h_codes[0][h][:], h_plane[0][h][:], h_bf0[h][:])
-            change1(TILES * h + 2)
-            if h == 1:
-                logits(1, 0, 2 * P)
-            change1(TILES * h + 3)
-            if h == 0:
-                logits(0, 0, HALF)
+        encode0(1, 0)
+        change0(0)
+        interleave0(0)
+        for j in range(TILES):
+            encode1(1, j)
+            encode0(1, 1, range(j, j + 1))
+            if j > 0:
+                change1(j - 1)
+            if j == 1:
+                quantize(h_codes[0][0][:], h_plane[0][0][:], h_bf0[0][:])
+        encode1(1, 4)
+        encode1(0, 5)
+        change1(3)
+        change0(1)
+        logits(0, 0, HALF)
+        encode1(1, 5)
+        encode1(0, 6)
+        change1(4)
+        interleave0(1)
+        encode1(1, 6)
+        encode1(0, 7)
+        change1(5)
+        quantize(h_codes[0][1][:], h_plane[0][1][:], h_bf0[1][:])
+        encode1(1, 7)
+        change1(6)
+        logits(1, 0, 2 * P)
+        change1(7)
         logits(1, 2 * P, P)
         logits(1, 3 * P, P)

@@ -97,11 +97,13 @@ def tile_list_replay_inverse_dynamics_kernel(
         def quantize(codes, plane, src):
             nc.vector.quantize_mx(out=codes.bitcast(FP8X4), scales=plane, in_=src.rearrange("p c i -> p (c i)"))
 
-        nc.scalar.activation(
-            w1_bf[0][:].rearrange("p (t m) i -> p m i t", t=PACK),
-            w1_raw[0][:].rearrange("p i (m t) -> p m i t", t=PACK),
-            ACT.Copy,
-        )
+        def cast_views(b, u):
+            dst = w1_bf[b][:].rearrange("p (u e m) i -> p u m e i", u=2, e=2)
+            src = w1_raw[b][:].rearrange("p i (m u e) -> p u m e i", u=2, e=2)
+            return dst[:, u], src[:, u]
+
+        for u in range(2):
+            nc.scalar.activation(*cast_views(0, u), ACT.Copy)
 
         enc0 = [[[held(f"enc0_{i}{h}{t}", [P, HALF], F32) for t in range(PACK)] for h in range(2)] for i in range(2)]
         enc1 = [{}, {}]
@@ -123,7 +125,7 @@ def tile_list_replay_inverse_dynamics_kernel(
 
         def encode1(i, j):
             h, cols = j // TILES, slice(P * (j % TILES), P * (j % TILES + 1))
-            enc1[i][j] = ring.tile([P, PACK, P], F32, name=f"enc1_{i}")
+            enc1[i][j] = ring.tile([P, PACK, P], F32, name=f"enc1_{i}", bufs=3 + i)
             z = zps.tile([P, PASS], F32, name="z")
             nc.tensor.matmul_mx(
                 out=z[:],
@@ -135,7 +137,7 @@ def tile_list_replay_inverse_dynamics_kernel(
                 stop=True,
             )
             nc.scalar.activation(
-                enc1[i][j][:], z[:].rearrange("p (m t) -> p t m", t=PACK), ACT.Tanh, scale=(-1.0 if i == 0 else 1.0)
+                enc1[i][j][:].rearrange("p t m -> p (t m)"), z[:], ACT.Tanh, scale=(-1.0 if i == 0 else 1.0)
             )
 
         scaled = [[held(f"scaled{h}{t}", [P, HALF], F32) for t in range(PACK)] for h in range(2)]
@@ -152,12 +154,11 @@ def tile_list_replay_inverse_dynamics_kernel(
         encode0(0, 0)
         gather_words(0, 1)
         encode0(0, 1)
-        nc.vector.tensor_copy(
-            w1_bf[1][:].rearrange("p (c e) i -> p c i e", e=4), w1_raw[1][:].rearrange("p i (c e) -> p c i e", e=4)
-        )
+        for u in range(2):
+            nc.vector.tensor_copy(*cast_views(1, u))
         prescale(0)
         quantize(w1_codes[1][:], w1_plane[1][:], w1_bf[1][:])
-        for j in range(TILES + 1):
+        for j in range(3):
             encode1(0, j)
         prescale(1)
         gather_words(1, 0)
@@ -220,26 +221,32 @@ def tile_list_replay_inverse_dynamics_kernel(
         encode0(1, 0)
         change0(0)
         interleave0(0)
-        for j in range(TILES):
-            encode1(1, j)
-            encode0(1, 1, range(j, j + 1))
-            if j > 0:
-                change1(j - 1)
-            if j == 1:
-                quantize(h_codes[0][0][:], h_plane[0][0][:], h_bf0[0][:])
+        encode1(1, 0)
+        encode0(1, 1, range(0, 1))
+        encode1(1, 1)
+        encode0(1, 1, range(1, 2))
+        change1(0)
+        quantize(h_codes[0][0][:], h_plane[0][0][:], h_bf0[0][:])
+        encode1(1, 2)
+        encode1(0, 3)
+        change1(1)
+        encode1(1, 3)
+        encode0(1, 1, range(2, 4))
+        change1(2)
+        encode1(0, 4)
         encode1(1, 4)
-        encode1(0, 5)
         change1(3)
         change0(1)
         logits(0, 0, HALF)
+        encode1(0, 5)
         encode1(1, 5)
-        encode1(0, 6)
         change1(4)
         interleave0(1)
+        encode1(0, 6)
         encode1(1, 6)
-        encode1(0, 7)
         change1(5)
         quantize(h_codes[0][1][:], h_plane[0][1][:], h_bf0[1][:])
+        encode1(0, 7)
         encode1(1, 7)
         change1(6)
         logits(1, 0, 2 * P)

@@ -48,31 +48,28 @@ def tile_list_replay_inverse_dynamics_kernel(
         ident = held("ident", [P, P], F32)
         warm = held("warm", [P, 8], F32)
 
-        nc.vector.memset(planes[0][:], 0)
-        nc.gpsimd.memset(planes[1][:], 0)
         nc.vector.memset(warm[:, 0:4], 0.0)
+        nc.vector.memset(planes[0][:], 0)
+        nc.vector.memset(planes[1][:], 0)
         nc.vector.memset(w4_plane[:], 0)
 
         def load_words(i, src):
             nc.sync.dma_start(words[i][:], src[0].rearrange("p t i -> p (t i)").bitcast(I32))
 
-        def load_plane(i, src, queue):
-            for r in range(4):
-                queue.dma_start(planes[i][4 * i + r : P : 32, :], src[0].bitcast(I32)[r:16:4, :])
-
         w1_rows = w1.rearrange("(p i) c -> p i c", i=PACK)
+        nc.gpsimd.dma_start(gains[:], gain.rearrange("(b p t) -> p b t", b=2, t=PACK))
+        with nc.allow_non_contiguous_dma(reason="one bias for each partition"):
+            nc.gpsimd.dma_start(biases[:], bias.rearrange("(c p) -> p c", p=P))
         nc.sync.dma_start(lists[0][:], offs)
-        nc.sync.dma_start(lists[1][:], offs2)
         nc.sync.dma_start(w1_raw[0][:], w1_rows[:, :, 0:PASS])
-        load_plane(0, tab_scales, nc.scalar)
+        nc.sync.dma_start(lists[1][:], offs2)
         nc.scalar.activation(warm[:, 4:8], warm[:, 0:4], ACT.Tanh)
-        load_plane(1, tab2_scales, nc.sync)
+        for r in range(4):
+            for i, src in enumerate((tab_scales, tab2_scales)):
+                nc.sync.dma_start(planes[i][4 * i + r : P : 32, :], src[0].bitcast(I32)[r:16:4, :])
         load_words(0, tab_words)
-        nc.sync.dma_start(gains[:], gain.rearrange("(b p t) -> p b t", b=2, t=PACK))
         nc.sync.dma_start(w1_raw[1][:], w1_rows[:, :, PASS : 2 * PASS])
         load_words(1, tab2_words)
-        with nc.allow_non_contiguous_dma(reason="one bias for each partition"):
-            nc.sync.dma_start(biases[:], bias.rearrange("(c p) -> p c", p=P))
         nc.sync.dma_start(w4_codes[:], w4_words.bitcast(I32).rearrange("a p c -> p a c"))
         for r in range(4):
             nc.sync.dma_start(
@@ -102,8 +99,8 @@ def tile_list_replay_inverse_dynamics_kernel(
             src = w1_raw[b][:].rearrange("p i (m u e) -> p u m e i", u=2, e=2)
             return dst[:, u], src[:, u]
 
-        for u in range(2):
-            nc.scalar.activation(*cast_views(0, u), ACT.Copy)
+        nc.scalar.activation(*cast_views(0, 0), ACT.Copy)
+        nc.vector.tensor_copy(*cast_views(0, 1))
 
         enc0 = [[[held(f"enc0_{i}{h}{t}", [P, HALF], F32) for t in range(PACK)] for h in range(2)] for i in range(2)]
         enc1 = [{}, {}]
@@ -125,7 +122,7 @@ def tile_list_replay_inverse_dynamics_kernel(
 
         def encode1(i, j):
             h, cols = j // TILES, slice(P * (j % TILES), P * (j % TILES + 1))
-            enc1[i][j] = ring.tile([P, PACK, P], F32, name=f"enc1_{i}", bufs=3 + i)
+            enc1[i][j] = ring.tile([P, PACK, P], F32, name=f"enc1_{i}", bufs=4)
             z = zps.tile([P, PASS], F32, name="z")
             nc.tensor.matmul_mx(
                 out=z[:],
@@ -158,7 +155,7 @@ def tile_list_replay_inverse_dynamics_kernel(
             nc.vector.tensor_copy(*cast_views(1, u))
         prescale(0)
         quantize(w1_codes[1][:], w1_plane[1][:], w1_bf[1][:])
-        for j in range(3):
+        for j in range(TILES):
             encode1(0, j)
         prescale(1)
         gather_words(1, 0)
@@ -171,19 +168,21 @@ def tile_list_replay_inverse_dynamics_kernel(
         h_plane = [[held(f"hplane{a}{h}", [P, HALF], U8) for h in range(2)] for a in range(2)]
         gain1 = gains[:, 1:2, :].to_broadcast([P, P, PACK])
 
-        def change0(h):
-            for t in range(PACK):
+        def change0(h, slots):
+            for t in slots:
                 nc.vector.scalar_tensor_tensor(
                     h_rows[h][:, t, :], enc0[1][h][t][:], gains[:, 0, t : t + 1], scaled[h][t][:], ALU.mult, ALU.subtract
                 )
 
-        def interleave0(h):
+        def interleave0(h, part):
+            cols = slice(2 * P * part, 2 * P * (part + 1))
             nc.vector.tensor_copy(
-                h_bf0[h][:].rearrange("p (c e) t -> p c t e", e=4), h_rows[h][:].rearrange("p t (c e) -> p c t e", e=4)
+                h_bf0[h][:, cols, :].rearrange("p (c e) t -> p c t e", e=4),
+                h_rows[h][:, :, cols].rearrange("p t (c e) -> p c t e", e=4),
             )
 
         def change1(j):
-            d = dps.tile([P, PACK, P], F32, name="d", tag="late")
+            d = dps.tile([P, PACK, P], F32, name="d")
             for t in range(PACK):
                 for i in range(2):
                     nc.tensor.matmul(
@@ -211,7 +210,7 @@ def tile_list_replay_inverse_dynamics_kernel(
             quantize(h_codes[1][h][:, cols], h_plane[1][h][:, cols], h_bf1[h][:, cols, :])
             res = held(f"res{h}_{first}", [P, 2, width], F32)
             for c in range(2):
-                acc = dps.tile([P, width], F32, name="acc", tag="late")
+                acc = zps.tile([P, width], F32, name="z")
                 step = HALF if width == HALF else P
                 for n0 in range(0, width, step):
                     product(acc[:, n0 : n0 + step], c, h, slice(first + n0, first + n0 + step))
@@ -219,36 +218,40 @@ def tile_list_replay_inverse_dynamics_kernel(
             nc.sync.dma_start(out_rows[:, :, HALF * h + first : HALF * h + first + width], res[:])
 
         encode0(1, 0)
-        change0(0)
-        interleave0(0)
+        change0(0, range(PACK))
         encode1(1, 0)
         encode0(1, 1, range(0, 1))
+        interleave0(0, 0)
         encode1(1, 1)
         encode0(1, 1, range(1, 2))
         change1(0)
-        quantize(h_codes[0][0][:], h_plane[0][0][:], h_bf0[0][:])
+        interleave0(0, 1)
         encode1(1, 2)
-        encode1(0, 3)
+        encode0(1, 1, range(2, 3))
         change1(1)
+        quantize(h_codes[0][0][:], h_plane[0][0][:], h_bf0[0][:])
         encode1(1, 3)
-        encode0(1, 1, range(2, 4))
+        encode0(1, 1, range(3, 4))
         change1(2)
+        change0(1, range(0, 2))
         encode1(0, 4)
         encode1(1, 4)
         change1(3)
-        change0(1)
-        logits(0, 0, HALF)
+        change0(1, range(2, 3))
         encode1(0, 5)
         encode1(1, 5)
+        logits(0, 0, HALF)
+        change0(1, range(3, 4))
         change1(4)
-        interleave0(1)
+        interleave0(1, 0)
         encode1(0, 6)
         encode1(1, 6)
         change1(5)
-        quantize(h_codes[0][1][:], h_plane[0][1][:], h_bf0[1][:])
+        interleave0(1, 1)
         encode1(0, 7)
         encode1(1, 7)
         change1(6)
+        quantize(h_codes[0][1][:], h_plane[0][1][:], h_bf0[1][:])
         logits(1, 0, 2 * P)
         change1(7)
         logits(1, 2 * P, P)

@@ -4,7 +4,7 @@ import concourse.mybir as mybir
 from concourse.masks import make_identity
 
 K, H, N, T, S = 512, 1024, 256, 4096, 1024
-FLOPS = 2 * K * H * S * 2 + 2 * H * N * S
+FLOPS = 2 * (2 * K * H * S) + 2 * H * N * S
 
 F32 = mybir.dt.float32
 BF16 = mybir.dt.bfloat16
@@ -20,8 +20,18 @@ ALU = mybir.AluOpType
 P = 128
 PACK = 4
 PASS = P * PACK
-HALF = 512
+HALF = S // 2
+QUARTER = S // 4
 TILES = HALF // P
+STRIPE = 16
+QUADRANT = 32
+SCALE_ROWS = 4
+STATES, SUCCESSORS = 0, 1
+DIRECT, TURNED = 0, 1
+SCALE_START = (0, 4)
+AHEAD = 5
+TURNED_BUFS = (AHEAD, 4)
+BANKS = 4
 
 
 def tile_list_replay_inverse_dynamics_kernel(
@@ -30,229 +40,248 @@ def tile_list_replay_inverse_dynamics_kernel(
     nc = tc.nc
     with ExitStack() as ctx:
         keep = ctx.enter_context(tc.tile_pool(name="keep", bufs=1))
-        ring = ctx.enter_context(tc.tile_pool(name="ring", bufs=5))
-        zps = ctx.enter_context(tc.psum_pool(name="zps", bufs=4))
-        dps = ctx.enter_context(tc.psum_pool(name="dps", bufs=4))
+        ring = ctx.enter_context(tc.tile_pool(name="ring", bufs=AHEAD))
+        mx_banks = ctx.enter_context(tc.psum_pool(name="mx_banks", bufs=BANKS))
+        turn_banks = ctx.enter_context(tc.psum_pool(name="turn_banks", bufs=BANKS))
 
         def held(name, shape, dtype):
             return keep.tile(shape, dtype, name=name, align_bytes=64)
 
-        lists = [keep.tile([P, S // 16], U16, name=f"list{i}") for i in range(2)]
-        words = [held(f"words{i}", [P, T], I32) for i in range(2)]
-        planes = [held(f"planes{i}", [P, T // 4], I32) for i in range(2)]
-        w1_raw = [held(f"w1raw{b}", [P, PACK, PASS], F32) for b in range(2)]
-        w4_codes = held("w4codes", [P, 2, 2 * N // 4], I32)
-        w4_plane = held("w4plane", [P, 2, N // 4], I32)
+        lists = [keep.tile([P, S // STRIPE], U16, name=f"list{i}") for i in range(2)]
+        table_words = [held(f"table_words{i}", [P, T], I32) for i in range(2)]
+        table_scales = [held(f"table_scales{i}", [P, T // 4], I32) for i in range(2)]
+        w1_raw = [held(f"w1_raw{g}", [P, PACK, PASS], F32) for g in range(2)]
+        w4_codes = held("w4_codes", [P, 2, N // 2], I32)
+        w4_scale = held("w4_scale", [P, 2, N // 4], I32)
         gains = held("gains", [P, 2, PACK], F32)
         biases = held("biases", [P, 2], F32)
         ident = held("ident", [P, P], F32)
-        warm = held("warm", [P, 8], F32)
 
-        nc.vector.memset(warm[:, 0:4], 0.0)
-        nc.vector.memset(planes[0][:], 0)
-        nc.vector.memset(planes[1][:], 0)
-        nc.vector.memset(w4_plane[:], 0)
+        nc.vector.memset(table_scales[STATES][:], 0)
+        nc.vector.memset(table_scales[SUCCESSORS][:], 0)
+        nc.vector.memset(w4_scale[:], 0)
 
         def load_words(i, src):
-            nc.sync.dma_start(words[i][:], src[0].rearrange("p t i -> p (t i)").bitcast(I32))
+            nc.sync.dma_start(table_words[i][:], src[0].rearrange("p t i -> p (t i)").bitcast(I32))
+
+        def load_scales(i, src):
+            for r in range(SCALE_ROWS):
+                nc.sync.dma_start(
+                    table_scales[i][SCALE_START[i] + r : P : QUADRANT, :], src[0].bitcast(I32)[r::SCALE_ROWS, :]
+                )
 
         w1_rows = w1.rearrange("(p i) c -> p i c", i=PACK)
-        nc.gpsimd.dma_start(gains[:], gain.rearrange("(b p t) -> p b t", b=2, t=PACK))
+        nc.gpsimd.dma_start(gains[:], gain.rearrange("(g p t) -> p g t", g=2, t=PACK))
         with nc.allow_non_contiguous_dma(reason="one bias for each partition"):
             nc.gpsimd.dma_start(biases[:], bias.rearrange("(c p) -> p c", p=P))
-        nc.sync.dma_start(lists[0][:], offs)
-        nc.sync.dma_start(w1_raw[0][:], w1_rows[:, :, 0:PASS])
-        nc.sync.dma_start(lists[1][:], offs2)
-        nc.scalar.activation(warm[:, 4:8], warm[:, 0:4], ACT.Tanh)
-        for r in range(4):
-            for i, src in enumerate((tab_scales, tab2_scales)):
-                nc.sync.dma_start(planes[i][4 * i + r : P : 32, :], src[0].bitcast(I32)[r:16:4, :])
-        load_words(0, tab_words)
-        nc.sync.dma_start(w1_raw[1][:], w1_rows[:, :, PASS : 2 * PASS])
-        load_words(1, tab2_words)
-        nc.sync.dma_start(w4_codes[:], w4_words.bitcast(I32).rearrange("a p c -> p a c"))
-        for r in range(4):
+        nc.sync.dma_start(lists[STATES][:], offs)
+        nc.sync.dma_start(w1_raw[DIRECT][:], w1_rows[:, :, 0:PASS])
+        load_scales(STATES, tab_scales)
+        load_words(STATES, tab_words)
+        nc.sync.dma_start(lists[SUCCESSORS][:], offs2)
+        load_scales(SUCCESSORS, tab2_scales)
+        nc.sync.dma_start(w1_raw[TURNED][:], w1_rows[:, :, PASS : 2 * PASS])
+        load_words(SUCCESSORS, tab2_words)
+        nc.sync.dma_start(w4_codes[:], w4_words.bitcast(I32).rearrange("g p c -> p g c"))
+        for r in range(SCALE_ROWS):
             nc.sync.dma_start(
-                w4_plane[r:P:32, :, :], w4_scales.bitcast(I32)[:, r:16:4, :].rearrange("a q c -> q a c")
+                w4_scale[r:P:QUADRANT, :, :], w4_scales.bitcast(I32)[:, r::SCALE_ROWS, :].rearrange("g q c -> q g c")
             )
         make_identity(nc, ident[:])
 
-        w1_bf = [held(f"w1bf{b}", [P, PASS, PACK], BF16) for b in range(2)]
-        w1_codes = [held(f"w1codes{b}", [P, PASS], U32) for b in range(2)]
-        w1_plane = [held(f"w1plane{b}", [P, PASS], U8) for b in range(2)]
-        picked_words = [[held(f"pw{i}{h}", [P, HALF], U32) for h in range(2)] for i in range(2)]
-        picked_plane = [[held(f"pp{i}{h}", [P, HALF], U8) for h in range(2)] for i in range(2)]
+        w1_bf = [held(f"w1_bf{g}", [P, PASS, PACK], BF16) for g in range(2)]
+        w1_codes = [held(f"w1_codes{g}", [P, PASS], U32) for g in range(2)]
+        w1_scale = [held(f"w1_scale{g}", [P, PASS], U8) for g in range(2)]
+        picked_words = [[held(f"picked_words{i}{h}", [P, HALF], U32) for h in range(2)] for i in range(2)]
+        picked_scales = [held(f"picked_scales{i}", [P, S], U8) for i in range(2)]
+        direct = [[[held(f"direct{i}{h}{t}", [P, HALF], F32) for t in range(PACK)] for h in range(2)] for i in range(2)]
+        turned = [{}, {}]
+        gained = [[held(f"gained{h}{t}", [P, HALF], F32) for t in range(PACK)] for h in range(2)]
+        h_slots = [held(f"h_slots{h}", [P, PACK, HALF], BF16) for h in range(2)]
+        h_bf = [[held(f"h_bf{g}{h}", [P, HALF, PACK], BF16) for h in range(2)] for g in range(2)]
+        h_codes = [[held(f"h_codes{g}{h}", [P, HALF], U32) for h in range(2)] for g in range(2)]
+        h_scale = [[held(f"h_scale{g}{h}", [P, HALF], U8) for h in range(2)] for g in range(2)]
+        turned_gain = gains[:, TURNED : TURNED + 1, :].to_broadcast([P, P, PACK])
+        out_rows = out.rearrange("(c p) j -> p c j", p=P)
 
         def gather_words(i, h):
-            offsets = lists[i][:, 32 * h : 32 * (h + 1)]
-            nc.vector.tensor_copy(picked_words[i][h][:], words[i][:].bitcast(U32).indirect(offsets))
+            offsets = lists[i][:, HALF * h // STRIPE : HALF * (h + 1) // STRIPE]
+            nc.vector.tensor_copy(picked_words[i][h][:], table_words[i][:].bitcast(U32).indirect(offsets))
 
-        def gather_plane(i, h):
-            offsets = lists[i][:, 32 * h : 32 * (h + 1)]
-            nc.vector.tensor_copy(picked_plane[i][h][:], planes[i][:].bitcast(U8).indirect(offsets))
+        def gather_scales(i, first, count):
+            offsets = lists[i][:, first // STRIPE : (first + count) // STRIPE]
+            nc.vector.tensor_copy(
+                picked_scales[i][:, first : first + count], table_scales[i][:].bitcast(U8).indirect(offsets)
+            )
 
-        def quantize(codes, plane, src):
-            nc.vector.quantize_mx(out=codes.bitcast(FP8X4), scales=plane, in_=src.rearrange("p c i -> p (c i)"))
-
-        def cast_views(b, u):
-            dst = w1_bf[b][:].rearrange("p (u e m) i -> p u m e i", u=2, e=2)
-            src = w1_raw[b][:].rearrange("p i (m u e) -> p u m e i", u=2, e=2)
+        def cast_views(g, u):
+            dst = w1_bf[g][:].rearrange("p (u e m) i -> p u m e i", u=2, e=2)
+            src = w1_raw[g][:].rearrange("p i (m u e) -> p u m e i", u=2, e=2)
             return dst[:, u], src[:, u]
 
-        nc.scalar.activation(*cast_views(0, 0), ACT.Copy)
-        nc.vector.tensor_copy(*cast_views(0, 1))
+        def quantize(codes, scale, src):
+            nc.vector.quantize_mx(out=codes.bitcast(FP8X4), scales=scale, in_=src.rearrange("p c i -> p (c i)"))
 
-        enc0 = [[[held(f"enc0_{i}{h}{t}", [P, HALF], F32) for t in range(PACK)] for h in range(2)] for i in range(2)]
-        enc1 = [{}, {}]
+        def quantize_w1(g):
+            quantize(w1_codes[g][:], w1_scale[g][:], w1_bf[g][:])
 
-        def encode0(i, h, slots=range(PACK)):
+        def quantize_h(g, h, first, width):
+            cols = slice(first, first + width)
+            quantize(h_codes[g][h][:, cols], h_scale[g][h][:, cols], h_bf[g][h][:, cols, :])
+
+        def encode_direct(i, h, slots):
             for t in slots:
-                z = zps.tile([P, HALF], F32, name="z")
+                z = mx_banks.tile([P, HALF], F32, name="mx_out")
                 cols = slice(P * t, P * (t + 1))
                 nc.tensor.matmul_mx(
                     out=z[:],
-                    lhsT=w1_codes[0][:, cols].bitcast(FP8X4),
-                    lhsT_scale=w1_plane[0][:, cols],
+                    lhsT=w1_codes[DIRECT][:, cols].bitcast(FP8X4),
+                    lhsT_scale=w1_scale[DIRECT][:, cols],
                     rhs=picked_words[i][h][:].bitcast(FP8X4),
-                    rhs_scale=picked_plane[i][h][4 * i : P, :],
+                    rhs_scale=picked_scales[i][SCALE_START[i] : P, HALF * h : HALF * (h + 1)],
                     start=True,
                     stop=True,
                 )
-                nc.scalar.activation(enc0[i][h][t][:], z[:], ACT.Tanh)
+                nc.scalar.activation(direct[i][h][t][:], z[:], ACT.Tanh)
 
-        def encode1(i, j):
+        def encode_turned(i, j):
             h, cols = j // TILES, slice(P * (j % TILES), P * (j % TILES + 1))
-            enc1[i][j] = ring.tile([P, PACK, P], F32, name=f"enc1_{i}", bufs=4)
-            z = zps.tile([P, PASS], F32, name="z")
+            turned[i][j] = ring.tile([P, PACK, P], F32, name=f"turned{i}", bufs=TURNED_BUFS[i])
+            z = mx_banks.tile([P, PASS], F32, name="mx_out")
             nc.tensor.matmul_mx(
                 out=z[:],
                 lhsT=picked_words[i][h][:, cols].bitcast(FP8X4),
-                lhsT_scale=picked_plane[i][h][4 * i : P, cols],
-                rhs=w1_codes[1][:].bitcast(FP8X4),
-                rhs_scale=w1_plane[1][:],
+                lhsT_scale=picked_scales[i][SCALE_START[i] : P, P * j : P * (j + 1)],
+                rhs=w1_codes[TURNED][:].bitcast(FP8X4),
+                rhs_scale=w1_scale[TURNED][:],
                 start=True,
                 stop=True,
             )
             nc.scalar.activation(
-                enc1[i][j][:].rearrange("p t m -> p (t m)"), z[:], ACT.Tanh, scale=(-1.0 if i == 0 else 1.0)
+                turned[i][j][:].rearrange("p t m -> p (t m)"), z[:], ACT.Tanh, scale=(-1.0 if i == STATES else 1.0)
             )
 
-        scaled = [[held(f"scaled{h}{t}", [P, HALF], F32) for t in range(PACK)] for h in range(2)]
-
-        def prescale(h):
+        def gain_states(h):
             for t in range(PACK):
-                nc.vector.tensor_scalar(scaled[h][t][:], enc0[0][h][t][:], gains[:, 0, t : t + 1], None, ALU.mult)
+                nc.gpsimd.tensor_scalar(
+                    gained[h][t][:], direct[STATES][h][t][:], gains[:, DIRECT, t : t + 1], 0.0, ALU.mult, ALU.add
+                )
 
-        for i in range(2):
-            for h in range(2):
-                gather_plane(i, h)
-        quantize(w1_codes[0][:], w1_plane[0][:], w1_bf[0][:])
-        gather_words(0, 0)
-        encode0(0, 0)
-        gather_words(0, 1)
-        encode0(0, 1)
-        for u in range(2):
-            nc.vector.tensor_copy(*cast_views(1, u))
-        prescale(0)
-        quantize(w1_codes[1][:], w1_plane[1][:], w1_bf[1][:])
-        for j in range(TILES):
-            encode1(0, j)
-        prescale(1)
-        gather_words(1, 0)
-        gather_words(1, 1)
-
-        h_rows = [held(f"hrows{h}", [P, PACK, HALF], BF16) for h in range(2)]
-        h_bf0 = [held(f"hbf0{h}", [P, HALF, PACK], BF16) for h in range(2)]
-        h_bf1 = [held(f"hbf1{h}", [P, HALF, PACK], BF16) for h in range(2)]
-        h_codes = [[held(f"hcodes{a}{h}", [P, HALF], U32) for h in range(2)] for a in range(2)]
-        h_plane = [[held(f"hplane{a}{h}", [P, HALF], U8) for h in range(2)] for a in range(2)]
-        gain1 = gains[:, 1:2, :].to_broadcast([P, P, PACK])
-
-        def change0(h, slots):
+        def change_direct(h, slots):
             for t in slots:
                 nc.vector.scalar_tensor_tensor(
-                    h_rows[h][:, t, :], enc0[1][h][t][:], gains[:, 0, t : t + 1], scaled[h][t][:], ALU.mult, ALU.subtract
+                    h_slots[h][:, t, :],
+                    direct[SUCCESSORS][h][t][:],
+                    gains[:, DIRECT, t : t + 1],
+                    gained[h][t][:],
+                    ALU.mult,
+                    ALU.subtract,
                 )
 
-        def interleave0(h, part):
-            cols = slice(2 * P * part, 2 * P * (part + 1))
+        def interleave_first_half(part):
+            cols = slice(QUARTER * part, QUARTER * (part + 1))
             nc.vector.tensor_copy(
-                h_bf0[h][:, cols, :].rearrange("p (c e) t -> p c t e", e=4),
-                h_rows[h][:, :, cols].rearrange("p t (c e) -> p c t e", e=4),
+                h_bf[DIRECT][0][:, cols, :].rearrange("p (c e) t -> p c t e", e=4),
+                h_slots[0][:, :, cols].rearrange("p t (c e) -> p c t e", e=4),
             )
 
-        def change1(j):
-            d = dps.tile([P, PACK, P], F32, name="d")
+        def interleave_second_half(part):
+            cols = slice(QUARTER * part, QUARTER * (part + 1))
+            nc.scalar.copy(h_bf[DIRECT][1][:, cols, :], h_slots[1][:, :, cols].rearrange("p t c -> p c t"))
+
+        def change_turned(j):
+            difference = turn_banks.tile([P, PACK, P], F32, name="difference")
             for t in range(PACK):
-                for i in range(2):
+                for i in (STATES, SUCCESSORS):
                     nc.tensor.matmul(
-                        d[:, t, :], enc1[i][j][:, t, :], ident[:], start=(i == 0), stop=(i == 1), is_transpose=True
+                        difference[:, t, :],
+                        turned[i][j][:, t, :],
+                        ident[:],
+                        start=(i == STATES),
+                        stop=(i == SUCCESSORS),
+                        is_transpose=True,
                     )
             cols = slice(P * (j % TILES), P * (j % TILES + 1))
-            nc.vector.tensor_tensor(h_bf1[j // TILES][:, cols, :], d[:].rearrange("p t j -> p j t"), gain1, ALU.mult)
+            nc.vector.tensor_tensor(
+                h_bf[TURNED][j // TILES][:, cols, :], difference[:].rearrange("p t j -> p j t"), turned_gain, ALU.mult
+            )
 
-        out_rows = out.rearrange("(c p) j -> p c j", p=P)
-
-        def product(acc, c, h, cols):
-            for a in range(2):
-                nc.tensor.matmul_mx(
-                    out=acc,
-                    lhsT=w4_codes[:, a, 64 * c : 64 * (c + 1)].bitcast(U8).bitcast(FP4X4),
-                    lhsT_scale=w4_plane[:, a, 32 * c : 32 * (c + 1)].bitcast(U8),
-                    rhs=h_codes[a][h][:, cols].bitcast(FP8X4),
-                    rhs_scale=h_plane[a][h][:, cols],
-                    start=(a == 0),
-                    stop=(a == 1),
-                )
-
-        def logits(h, first, width):
-            cols = slice(first, first + width)
-            quantize(h_codes[1][h][:, cols], h_plane[1][h][:, cols], h_bf1[h][:, cols, :])
-            res = held(f"res{h}_{first}", [P, 2, width], F32)
+        def logits(h, first, width, shared):
+            result = held(f"result{h}_{first}", [P, 2, width], F32)
+            tokens = slice(HALF * h + first, HALF * h + first + width)
+            step = HALF if width == HALF else P
             for c in range(2):
-                acc = zps.tile([P, width], F32, name="z")
-                step = HALF if width == HALF else P
+                acc = mx_banks.tile([P, width], F32, name="mx_out")
                 for n0 in range(0, width, step):
-                    product(acc[:, n0 : n0 + step], c, h, slice(first + n0, first + n0 + step))
-                nc.scalar.activation(res[:, c, :], acc[:], ACT.Identity, bias=biases[:, c : c + 1])
-            nc.sync.dma_start(out_rows[:, :, HALF * h + first : HALF * h + first + width], res[:])
+                    cols = slice(first + n0, first + n0 + step)
+                    for g in (DIRECT, TURNED):
+                        nc.tensor.matmul_mx(
+                            out=acc[:, n0 : n0 + step],
+                            lhsT=w4_codes[:, g, P // 2 * c : P // 2 * (c + 1)].bitcast(U8).bitcast(FP4X4),
+                            lhsT_scale=w4_scale[:, g, P // 4 * c : P // 4 * (c + 1)].bitcast(U8),
+                            rhs=h_codes[g][h][:, cols].bitcast(FP8X4),
+                            rhs_scale=h_scale[g][h][:, cols],
+                            start=(g == DIRECT),
+                            stop=(g == TURNED),
+                        )
+                if shared and c == 1:
+                    nc.vector.tensor_scalar(result[:, c, :], acc[:], biases[:, c : c + 1], None, ALU.add)
+                else:
+                    nc.scalar.activation(result[:, c, :], acc[:], ACT.Identity, bias=biases[:, c : c + 1])
+                nc.sync.dma_start(out_rows[:, c, tokens], result[:, c, :])
 
-        encode0(1, 0)
-        change0(0, range(PACK))
-        encode1(1, 0)
-        encode0(1, 1, range(0, 1))
-        interleave0(0, 0)
-        encode1(1, 1)
-        encode0(1, 1, range(1, 2))
-        change1(0)
-        interleave0(0, 1)
-        encode1(1, 2)
-        encode0(1, 1, range(2, 3))
-        change1(1)
-        quantize(h_codes[0][0][:], h_plane[0][0][:], h_bf0[0][:])
-        encode1(1, 3)
-        encode0(1, 1, range(3, 4))
-        change1(2)
-        change0(1, range(0, 2))
-        encode1(0, 4)
-        encode1(1, 4)
-        change1(3)
-        change0(1, range(2, 3))
-        encode1(0, 5)
-        encode1(1, 5)
-        logits(0, 0, HALF)
-        change0(1, range(3, 4))
-        change1(4)
-        interleave0(1, 0)
-        encode1(0, 6)
-        encode1(1, 6)
-        change1(5)
-        interleave0(1, 1)
-        encode1(0, 7)
-        encode1(1, 7)
-        change1(6)
-        quantize(h_codes[0][1][:], h_plane[0][1][:], h_bf0[1][:])
-        logits(1, 0, 2 * P)
-        change1(7)
-        logits(1, 2 * P, P)
-        logits(1, 3 * P, P)
+        nc.scalar.activation(*cast_views(DIRECT, 0), ACT.Copy)
+        nc.vector.tensor_copy(*cast_views(DIRECT, 1))
+        gather_scales(STATES, 0, S)
+        quantize_w1(DIRECT)
+        for h in range(2):
+            gather_words(STATES, h)
+            encode_direct(STATES, h, range(PACK))
+        gather_scales(SUCCESSORS, 0, HALF)
+        for u in range(2):
+            nc.vector.tensor_copy(*cast_views(TURNED, u))
+        gain_states(0)
+        quantize_w1(TURNED)
+        gather_scales(SUCCESSORS, HALF, HALF)
+        for j in range(AHEAD):
+            encode_turned(STATES, j)
+        gain_states(1)
+
+        gather_words(SUCCESSORS, 0)
+        gather_words(SUCCESSORS, 1)
+        encode_direct(SUCCESSORS, 0, range(PACK))
+        change_direct(0, range(PACK))
+        encode_turned(SUCCESSORS, 0)
+        encode_direct(SUCCESSORS, 1, [0])
+        interleave_first_half(0)
+        encode_turned(SUCCESSORS, 1)
+        encode_direct(SUCCESSORS, 1, [1])
+        change_turned(0)
+        interleave_first_half(1)
+        encode_turned(SUCCESSORS, 2)
+        encode_direct(SUCCESSORS, 1, [2])
+        change_turned(1)
+        quantize_h(DIRECT, 0, 0, HALF)
+        encode_turned(SUCCESSORS, 3)
+        encode_direct(SUCCESSORS, 1, [3])
+        change_turned(2)
+        change_direct(1, [0, 1])
+        encode_turned(SUCCESSORS, 4)
+        change_turned(3)
+        change_direct(1, [2, 3])
+        quantize_h(TURNED, 0, 0, HALF)
+        for j in range(AHEAD, 2 * TILES):
+            encode_turned(STATES, j)
+            encode_turned(SUCCESSORS, j)
+        for j in range(TILES, 2 * TILES - 1):
+            change_turned(j)
+        interleave_second_half(0)
+        interleave_second_half(1)
+        logits(0, 0, HALF, shared=False)
+        quantize_h(TURNED, 1, 0, QUARTER)
+        change_turned(2 * TILES - 1)
+        quantize_h(DIRECT, 1, 0, QUARTER)
+        logits(1, 0, QUARTER, shared=False)
+        quantize_h(TURNED, 1, QUARTER, QUARTER)
+        quantize_h(DIRECT, 1, QUARTER, QUARTER)
+        logits(1, QUARTER, QUARTER, shared=True)

@@ -28,10 +28,10 @@ QUADRANT = 32
 SCALE_ROWS = 4
 STATES, SUCCESSORS = 0, 1
 DIRECT, TURNED = 0, 1
+STAGE_ROWS = (slice(112, 128), slice(4, 128, 8))
 SCALE_START = (0, 4)
-AHEAD = 5
-TURNED_BUFS = (AHEAD, 4)
 BANKS = 4
+TURNED_BUFS = 4
 
 
 def tile_list_replay_inverse_dynamics_kernel(
@@ -40,62 +40,65 @@ def tile_list_replay_inverse_dynamics_kernel(
     nc = tc.nc
     with ExitStack() as ctx:
         keep = ctx.enter_context(tc.tile_pool(name="keep", bufs=1))
-        ring = ctx.enter_context(tc.tile_pool(name="ring", bufs=AHEAD))
+        ring = ctx.enter_context(tc.tile_pool(name="ring", bufs=TURNED_BUFS))
         mx_banks = ctx.enter_context(tc.psum_pool(name="mx_banks", bufs=BANKS))
         turn_banks = ctx.enter_context(tc.psum_pool(name="turn_banks", bufs=BANKS))
 
-        def held(name, shape, dtype):
-            return keep.tile(shape, dtype, name=name, align_bytes=64)
+        def held(name, shape, dtype, on=None):
+            return keep.tile(shape, dtype, name=name, tag=on or name, align_bytes=64)
 
         lists = [keep.tile([P, S // STRIPE], U16, name=f"list{i}") for i in range(2)]
-        table_words = [held(f"table_words{i}", [P, T], I32) for i in range(2)]
-        table_scales = [held(f"table_scales{i}", [P, T // 4], I32) for i in range(2)]
-        w1_raw = [held(f"w1_raw{g}", [P, PACK, PASS], F32) for g in range(2)]
-        w4_codes = held("w4_codes", [P, 2, N // 2], I32)
-        w4_scale = held("w4_scale", [P, 2, N // 4], I32)
+        staged_scales = [held(f"staged_scales{i}", [P, T // 4], I32) for i in range(2)]
+        picked_rows = [held(f"picked_rows{i}", [P, S], U8) for i in range(2)]
         gains = held("gains", [P, 2, PACK], F32)
         biases = held("biases", [P, 2], F32)
         ident = held("ident", [P, P], F32)
+        table_words, w1_raw, picked_scales, w4 = {}, {}, {}, {}
+        w1_rows = w1.rearrange("(p i) c -> p i c", i=PACK)
 
-        nc.vector.memset(table_scales[STATES][:], 0)
-        nc.vector.memset(table_scales[SUCCESSORS][:], 0)
-        nc.vector.memset(w4_scale[:], 0)
-
-        def load_words(i, src):
+        def load_words(i, src, on=None):
+            table_words[i] = held(f"table_words{i}", [P, T], I32, on)
             nc.sync.dma_start(table_words[i][:], src[0].rearrange("p t i -> p (t i)").bitcast(I32))
 
+        def load_w1(g, on=None):
+            w1_raw[g] = held(f"w1_raw{g}", [P, PACK, PASS], F32, on)
+            nc.sync.dma_start(w1_raw[g][:], w1_rows[:, :, PASS * g : PASS * (g + 1)])
+
         def load_scales(i, src):
+            nc.sync.dma_start(staged_scales[i][STAGE_ROWS[i], :], src[0].bitcast(I32))
+
+        def gather_scales(i):
+            nc.vector.tensor_copy(picked_rows[i][:], staged_scales[i][:].bitcast(U8).indirect(lists[i][:]))
+
+        def place_scales(i, on=None):
+            picked_scales[i] = held(f"picked_scales{i}", [P, S // 4], I32, on)
+            nc.vector.memset(picked_scales[i][:], 0)
+            rows = STAGE_ROWS[i]
+            step = rows.step or 1
             for r in range(SCALE_ROWS):
                 nc.sync.dma_start(
-                    table_scales[i][SCALE_START[i] + r : P : QUADRANT, :], src[0].bitcast(I32)[r::SCALE_ROWS, :]
+                    picked_scales[i][SCALE_START[i] + r : P : QUADRANT, :],
+                    picked_rows[i][rows.start + step * r : P : step * SCALE_ROWS, :].bitcast(I32),
                 )
 
-        w1_rows = w1.rearrange("(p i) c -> p i c", i=PACK)
-        nc.gpsimd.dma_start(gains[:], gain.rearrange("(g p t) -> p g t", g=2, t=PACK))
-        with nc.allow_non_contiguous_dma(reason="one bias for each partition"):
-            nc.gpsimd.dma_start(biases[:], bias.rearrange("(c p) -> p c", p=P))
-        nc.sync.dma_start(lists[STATES][:], offs)
-        nc.sync.dma_start(w1_raw[DIRECT][:], w1_rows[:, :, 0:PASS])
-        load_scales(STATES, tab_scales)
-        load_words(STATES, tab_words)
-        nc.sync.dma_start(lists[SUCCESSORS][:], offs2)
-        load_scales(SUCCESSORS, tab2_scales)
-        nc.sync.dma_start(w1_raw[TURNED][:], w1_rows[:, :, PASS : 2 * PASS])
-        load_words(SUCCESSORS, tab2_words)
-        nc.sync.dma_start(w4_codes[:], w4_words.bitcast(I32).rearrange("g p c -> p g c"))
-        for r in range(SCALE_ROWS):
-            nc.sync.dma_start(
-                w4_scale[r:P:QUADRANT, :, :], w4_scales.bitcast(I32)[:, r::SCALE_ROWS, :].rearrange("g q c -> q g c")
-            )
-        make_identity(nc, ident[:])
+        def load_w4():
+            w4["codes"] = held("w4_codes", [P, 2, N // 2], I32, "staged_scales0")
+            w4["scale"] = held("w4_scale", [P, 2, N // 4], I32, "w1_bf1")
+            nc.vector.memset(w4["scale"][:], 0)
+            nc.sync.dma_start(w4["codes"][:], w4_words.bitcast(I32).rearrange("g p c -> p g c"))
+            for r in range(SCALE_ROWS):
+                nc.sync.dma_start(
+                    w4["scale"][r:P:QUADRANT, :, :],
+                    w4_scales.bitcast(I32)[:, r::SCALE_ROWS, :].rearrange("g q c -> q g c"),
+                )
 
         w1_bf = [held(f"w1_bf{g}", [P, PASS, PACK], BF16) for g in range(2)]
         w1_codes = [held(f"w1_codes{g}", [P, PASS], U32) for g in range(2)]
         w1_scale = [held(f"w1_scale{g}", [P, PASS], U8) for g in range(2)]
         picked_words = [[held(f"picked_words{i}{h}", [P, HALF], U32) for h in range(2)] for i in range(2)]
-        picked_scales = [held(f"picked_scales{i}", [P, S], U8) for i in range(2)]
         direct = [[[held(f"direct{i}{h}{t}", [P, HALF], F32) for t in range(PACK)] for h in range(2)] for i in range(2)]
         turned = [{}, {}]
+        difference = {}
         gained = [[held(f"gained{h}{t}", [P, HALF], F32) for t in range(PACK)] for h in range(2)]
         h_slots = [held(f"h_slots{h}", [P, PACK, HALF], BF16) for h in range(2)]
         h_bf = [[held(f"h_bf{g}{h}", [P, HALF, PACK], BF16) for h in range(2)] for g in range(2)]
@@ -104,15 +107,12 @@ def tile_list_replay_inverse_dynamics_kernel(
         turned_gain = gains[:, TURNED : TURNED + 1, :].to_broadcast([P, P, PACK])
         out_rows = out.rearrange("(c p) j -> p c j", p=P)
 
+        def scale_plane(i, first, count):
+            return picked_scales[i][SCALE_START[i] : P, :].bitcast(U8)[:, first : first + count]
+
         def gather_words(i, h):
             offsets = lists[i][:, HALF * h // STRIPE : HALF * (h + 1) // STRIPE]
             nc.vector.tensor_copy(picked_words[i][h][:], table_words[i][:].bitcast(U32).indirect(offsets))
-
-        def gather_scales(i, first, count):
-            offsets = lists[i][:, first // STRIPE : (first + count) // STRIPE]
-            nc.vector.tensor_copy(
-                picked_scales[i][:, first : first + count], table_scales[i][:].bitcast(U8).indirect(offsets)
-            )
 
         def cast_views(g, u):
             dst = w1_bf[g][:].rearrange("p (u e m) i -> p u m e i", u=2, e=2)
@@ -138,7 +138,7 @@ def tile_list_replay_inverse_dynamics_kernel(
                     lhsT=w1_codes[DIRECT][:, cols].bitcast(FP8X4),
                     lhsT_scale=w1_scale[DIRECT][:, cols],
                     rhs=picked_words[i][h][:].bitcast(FP8X4),
-                    rhs_scale=picked_scales[i][SCALE_START[i] : P, HALF * h : HALF * (h + 1)],
+                    rhs_scale=scale_plane(i, HALF * h, HALF),
                     start=True,
                     stop=True,
                 )
@@ -146,12 +146,12 @@ def tile_list_replay_inverse_dynamics_kernel(
 
         def encode_turned(i, j):
             h, cols = j // TILES, slice(P * (j % TILES), P * (j % TILES + 1))
-            turned[i][j] = ring.tile([P, PACK, P], F32, name=f"turned{i}", bufs=TURNED_BUFS[i])
+            turned[i][j] = ring.tile([P, PACK, P], F32, name=f"turned{i}")
             z = mx_banks.tile([P, PASS], F32, name="mx_out")
             nc.tensor.matmul_mx(
                 out=z[:],
                 lhsT=picked_words[i][h][:, cols].bitcast(FP8X4),
-                lhsT_scale=picked_scales[i][SCALE_START[i] : P, P * j : P * (j + 1)],
+                lhsT_scale=scale_plane(i, P * j, P),
                 rhs=w1_codes[TURNED][:].bitcast(FP8X4),
                 rhs_scale=w1_scale[TURNED][:],
                 start=True,
@@ -163,9 +163,7 @@ def tile_list_replay_inverse_dynamics_kernel(
 
         def gain_states(h):
             for t in range(PACK):
-                nc.gpsimd.tensor_scalar(
-                    gained[h][t][:], direct[STATES][h][t][:], gains[:, DIRECT, t : t + 1], 0.0, ALU.mult, ALU.add
-                )
+                nc.vector.tensor_scalar(gained[h][t][:], direct[STATES][h][t][:], gains[:, DIRECT, t : t + 1], None, ALU.mult)
 
         def change_direct(h, slots):
             for t in slots:
@@ -178,110 +176,139 @@ def tile_list_replay_inverse_dynamics_kernel(
                     ALU.subtract,
                 )
 
-        def interleave_first_half(part):
+        def interleave(h, part):
             cols = slice(QUARTER * part, QUARTER * (part + 1))
             nc.vector.tensor_copy(
-                h_bf[DIRECT][0][:, cols, :].rearrange("p (c e) t -> p c t e", e=4),
-                h_slots[0][:, :, cols].rearrange("p t (c e) -> p c t e", e=4),
+                h_bf[DIRECT][h][:, cols, :].rearrange("p (c e) t -> p c t e", e=4),
+                h_slots[h][:, :, cols].rearrange("p t (c e) -> p c t e", e=4),
             )
 
-        def interleave_second_half(part):
-            cols = slice(QUARTER * part, QUARTER * (part + 1))
-            nc.scalar.copy(h_bf[DIRECT][1][:, cols, :], h_slots[1][:, :, cols].rearrange("p t c -> p c t"))
+        def turn(i, j):
+            if i == STATES:
+                difference[j] = turn_banks.tile([P, PACK, P], F32, name="difference")
+            for t in range(PACK):
+                nc.tensor.matmul(
+                    difference[j][:, t, :],
+                    turned[i][j][:, t, :],
+                    ident[:],
+                    start=(i == STATES and t == 0),
+                    stop=(i == SUCCESSORS and t == PACK - 1),
+                    is_transpose=True,
+                )
 
         def change_turned(j):
-            difference = turn_banks.tile([P, PACK, P], F32, name="difference")
-            for t in range(PACK):
-                for i in (STATES, SUCCESSORS):
-                    nc.tensor.matmul(
-                        difference[:, t, :],
-                        turned[i][j][:, t, :],
-                        ident[:],
-                        start=(i == STATES),
-                        stop=(i == SUCCESSORS),
-                        is_transpose=True,
-                    )
             cols = slice(P * (j % TILES), P * (j % TILES + 1))
             nc.vector.tensor_tensor(
-                h_bf[TURNED][j // TILES][:, cols, :], difference[:].rearrange("p t j -> p j t"), turned_gain, ALU.mult
+                h_bf[TURNED][j // TILES][:, cols, :], difference[j][:].rearrange("p t j -> p j t"), turned_gain, ALU.mult
             )
 
         def logits(h, first, width, shared):
-            result = held(f"result{h}_{first}", [P, 2, width], F32)
             tokens = slice(HALF * h + first, HALF * h + first + width)
             step = HALF if width == HALF else P
             for c in range(2):
+                result = held(f"result{h}_{first}_{c}", [P, width], F32)
                 acc = mx_banks.tile([P, width], F32, name="mx_out")
                 for n0 in range(0, width, step):
                     cols = slice(first + n0, first + n0 + step)
                     for g in (DIRECT, TURNED):
                         nc.tensor.matmul_mx(
                             out=acc[:, n0 : n0 + step],
-                            lhsT=w4_codes[:, g, P // 2 * c : P // 2 * (c + 1)].bitcast(U8).bitcast(FP4X4),
-                            lhsT_scale=w4_scale[:, g, P // 4 * c : P // 4 * (c + 1)].bitcast(U8),
+                            lhsT=w4["codes"][:, g, P // 2 * c : P // 2 * (c + 1)].bitcast(U8).bitcast(FP4X4),
+                            lhsT_scale=w4["scale"][:, g, P // 4 * c : P // 4 * (c + 1)].bitcast(U8),
                             rhs=h_codes[g][h][:, cols].bitcast(FP8X4),
                             rhs_scale=h_scale[g][h][:, cols],
                             start=(g == DIRECT),
                             stop=(g == TURNED),
                         )
                 if shared and c == 1:
-                    nc.vector.tensor_scalar(result[:, c, :], acc[:], biases[:, c : c + 1], None, ALU.add)
+                    nc.vector.tensor_scalar(result[:], acc[:], biases[:, c : c + 1], None, ALU.add)
                 else:
-                    nc.scalar.activation(result[:, c, :], acc[:], ACT.Identity, bias=biases[:, c : c + 1])
-                nc.sync.dma_start(out_rows[:, c, tokens], result[:, c, :])
+                    nc.scalar.activation(result[:], acc[:], ACT.Identity, bias=biases[:, c : c + 1])
+                nc.sync.dma_start(out_rows[:, c, tokens], result[:])
 
+        nc.vector.memset(staged_scales[STATES][0 : STAGE_ROWS[STATES].start, :], 0)
+        nc.vector.memset(staged_scales[SUCCESSORS][:], 0)
+        nc.sync.dma_start(lists[STATES][:], offs)
+        load_scales(STATES, tab_scales)
+        nc.sync.dma_start(lists[SUCCESSORS][:], offs2)
+        load_w1(DIRECT)
+        load_scales(SUCCESSORS, tab2_scales)
+        load_words(STATES, tab_words)
+        nc.gpsimd.dma_start(gains[:], gain.rearrange("(g p t) -> p g t", g=2, t=PACK))
+        with nc.allow_non_contiguous_dma(reason="one bias for each partition"):
+            nc.gpsimd.dma_start(biases[:], bias.rearrange("(c p) -> p c", p=P))
+        make_identity(nc, ident[:])
+
+        gather_scales(STATES)
+        place_scales(STATES)
+        load_w1(TURNED, on="staged_scales0")
         nc.scalar.activation(*cast_views(DIRECT, 0), ACT.Copy)
         nc.vector.tensor_copy(*cast_views(DIRECT, 1))
-        gather_scales(STATES, 0, S)
+        load_words(SUCCESSORS, tab2_words, on="w1_raw0")
+        gather_scales(SUCCESSORS)
         quantize_w1(DIRECT)
+        place_scales(SUCCESSORS, on="w1_bf0")
         for h in range(2):
             gather_words(STATES, h)
             encode_direct(STATES, h, range(PACK))
-        gather_scales(SUCCESSORS, 0, HALF)
         for u in range(2):
             nc.vector.tensor_copy(*cast_views(TURNED, u))
-        gain_states(0)
         quantize_w1(TURNED)
-        gather_scales(SUCCESSORS, HALF, HALF)
-        for j in range(AHEAD):
-            encode_turned(STATES, j)
+        load_w4()
+        gain_states(0)
         gain_states(1)
-
+        for j in range(3):
+            encode_turned(STATES, j)
         gather_words(SUCCESSORS, 0)
         gather_words(SUCCESSORS, 1)
+        for j in range(3):
+            turn(STATES, j)
+
         encode_direct(SUCCESSORS, 0, range(PACK))
         change_direct(0, range(PACK))
-        encode_turned(SUCCESSORS, 0)
-        encode_direct(SUCCESSORS, 1, [0])
-        interleave_first_half(0)
-        encode_turned(SUCCESSORS, 1)
-        encode_direct(SUCCESSORS, 1, [1])
-        change_turned(0)
-        interleave_first_half(1)
-        encode_turned(SUCCESSORS, 2)
-        encode_direct(SUCCESSORS, 1, [2])
-        change_turned(1)
-        quantize_h(DIRECT, 0, 0, HALF)
+        for j in range(3):
+            encode_turned(SUCCESSORS, j)
+        encode_turned(STATES, 3)
         encode_turned(SUCCESSORS, 3)
-        encode_direct(SUCCESSORS, 1, [3])
+        interleave(0, 0)
+        interleave(0, 1)
+        for j in range(3):
+            turn(SUCCESSORS, j)
+        change_turned(0)
+        quantize_h(DIRECT, 0, 0, HALF)
+        change_turned(1)
         change_turned(2)
-        change_direct(1, [0, 1])
-        encode_turned(SUCCESSORS, 4)
+        encode_direct(SUCCESSORS, 1, [0, 1])
+        turn(STATES, 3)
+        turn(SUCCESSORS, 3)
         change_turned(3)
-        change_direct(1, [2, 3])
+        encode_direct(SUCCESSORS, 1, [2, 3])
+        change_direct(1, [0])
         quantize_h(TURNED, 0, 0, HALF)
-        for j in range(AHEAD, 2 * TILES):
+        change_direct(1, [1, 2, 3])
+
+        for j in (4, 5):
             encode_turned(STATES, j)
             encode_turned(SUCCESSORS, j)
-        for j in range(TILES, 2 * TILES - 1):
-            change_turned(j)
-        interleave_second_half(0)
-        interleave_second_half(1)
         logits(0, 0, HALF, shared=False)
+        interleave(1, 0)
+        interleave(1, 1)
+        for j in (4, 5):
+            turn(STATES, j)
+            turn(SUCCESSORS, j)
+        for j in (6, 7):
+            encode_turned(STATES, j)
+        for j in (6, 7):
+            encode_turned(SUCCESSORS, j)
+        change_turned(4)
+        quantize_h(DIRECT, 1, 0, HALF)
+        change_turned(5)
+        for i in (STATES, SUCCESSORS):
+            for j in (6, 7):
+                turn(i, j)
+        change_turned(6)
         quantize_h(TURNED, 1, 0, QUARTER)
-        change_turned(2 * TILES - 1)
-        quantize_h(DIRECT, 1, 0, QUARTER)
+        change_turned(7)
         logits(1, 0, QUARTER, shared=False)
         quantize_h(TURNED, 1, QUARTER, QUARTER)
-        quantize_h(DIRECT, 1, QUARTER, QUARTER)
         logits(1, QUARTER, QUARTER, shared=True)

@@ -32,6 +32,7 @@ STAGE_ROWS = (slice(112, 128), slice(4, 128, 8))
 SCALE_START = (0, 4)
 BANKS = 4
 TURNED_BUFS = 4
+AHEAD = 2
 
 
 def tile_list_replay_inverse_dynamics_kernel(
@@ -83,7 +84,7 @@ def tile_list_replay_inverse_dynamics_kernel(
 
         def load_w4():
             w4["codes"] = held("w4_codes", [P, 2, N // 2], I32, "staged_scales0")
-            w4["scale"] = held("w4_scale", [P, 2, N // 4], I32, "w1_bf1")
+            w4["scale"] = held("w4_scale", [P, 2, N // 4], I32, "picked_rows1")
             nc.vector.memset(w4["scale"][:], 0)
             nc.sync.dma_start(w4["codes"][:], w4_words.bitcast(I32).rearrange("g p c -> p g c"))
             for r in range(SCALE_ROWS):
@@ -99,7 +100,7 @@ def tile_list_replay_inverse_dynamics_kernel(
         direct = [[[held(f"direct{i}{h}{t}", [P, HALF], F32) for t in range(PACK)] for h in range(2)] for i in range(2)]
         turned = [{}, {}]
         difference = {}
-        gained = [[held(f"gained{h}{t}", [P, HALF], F32) for t in range(PACK)] for h in range(2)]
+        gained = {}
         h_slots = [held(f"h_slots{h}", [P, PACK, HALF], BF16) for h in range(2)]
         h_bf = [[held(f"h_bf{g}{h}", [P, HALF, PACK], BF16) for h in range(2)] for g in range(2)]
         h_codes = [[held(f"h_codes{g}{h}", [P, HALF], U32) for h in range(2)] for g in range(2)]
@@ -118,6 +119,11 @@ def tile_list_replay_inverse_dynamics_kernel(
             dst = w1_bf[g][:].rearrange("p (u e m) i -> p u m e i", u=2, e=2)
             src = w1_raw[g][:].rearrange("p i (m u e) -> p u m e i", u=2, e=2)
             return dst[:, u], src[:, u]
+
+        def cast_turned(u):
+            dst = w1_bf[TURNED][:].rearrange("p (q u e m) i -> p u q m e i", q=2, u=2, e=2)
+            src = w1_raw[TURNED][:].rearrange("p i (q m u e) -> p u q m e i", q=2, u=2, e=2)
+            nc.vector.tensor_copy(dst[:, u], src[:, u])
 
         def quantize(codes, scale, src):
             nc.vector.quantize_mx(out=codes.bitcast(FP8X4), scales=scale, in_=src.rearrange("p c i -> p (c i)"))
@@ -144,26 +150,45 @@ def tile_list_replay_inverse_dynamics_kernel(
                 )
                 nc.scalar.activation(direct[i][h][t][:], z[:], ACT.Tanh)
 
-        def encode_turned(i, j):
-            h, cols = j // TILES, slice(P * (j % TILES), P * (j % TILES + 1))
-            turned[i][j] = ring.tile([P, PACK, P], F32, name=f"turned{i}")
-            z = mx_banks.tile([P, PASS], F32, name="mx_out")
-            nc.tensor.matmul_mx(
-                out=z[:],
-                lhsT=picked_words[i][h][:, cols].bitcast(FP8X4),
-                lhsT_scale=scale_plane(i, P * j, P),
-                rhs=w1_codes[TURNED][:].bitcast(FP8X4),
-                rhs_scale=w1_scale[TURNED][:],
-                start=True,
-                stop=True,
-            )
-            nc.scalar.activation(
-                turned[i][j][:].rearrange("p t m -> p (t m)"), z[:], ACT.Tanh, scale=(-1.0 if i == STATES else 1.0)
-            )
+        def encode_turned(i, pair):
+            if i == SUCCESSORS:
+                both = ring.tile([P, 2, PACK, P], F32, name="turned_successors")[:]
+            elif pair < AHEAD:
+                both = held(f"turned_states{pair}", [P, 2, PACK, P], F32)[:]
+            else:
+                if pair == AHEAD:
+                    w4["late"] = held("late_states", [P, TILES - AHEAD, 2, PACK, P], F32, "w1_raw0")
+                both = w4["late"][:, pair - AHEAD]
+            for e in range(2):
+                turned[i][2 * pair + e] = both[:, e]
+            for q in range(2):
+                cols = slice(PASS // 2 * q, PASS // 2 * (q + 1))
+                z = mx_banks.tile([P, 2, PASS // 2], F32, name="mx_out")
+                for e in range(2):
+                    j = 2 * pair + e
+                    nc.tensor.matmul_mx(
+                        out=z[:, e, :],
+                        lhsT=picked_words[i][j // TILES][:, P * (j % TILES) : P * (j % TILES + 1)].bitcast(FP8X4),
+                        lhsT_scale=scale_plane(i, P * j, P),
+                        rhs=w1_codes[TURNED][:, cols].bitcast(FP8X4),
+                        rhs_scale=w1_scale[TURNED][:, cols],
+                        start=True,
+                        stop=True,
+                    )
+                nc.scalar.activation(
+                    both[:, :, :, P // 2 * q : P // 2 * (q + 1)],
+                    z[:].rearrange("p e (t m) -> p e t m", t=PACK),
+                    ACT.Tanh,
+                    scale=(-1.0 if i == STATES else 1.0),
+                )
 
         def gain_states(h):
+            if h == 0:
+                both = held("gained", [P, 2, PACK, HALF], F32, "w1_bf1")
+                for k in range(2):
+                    gained[k] = [both[:, k, t, :] for t in range(PACK)]
             for t in range(PACK):
-                nc.vector.tensor_scalar(gained[h][t][:], direct[STATES][h][t][:], gains[:, DIRECT, t : t + 1], None, ALU.mult)
+                nc.vector.tensor_scalar(gained[h][t], direct[STATES][h][t][:], gains[:, DIRECT, t : t + 1], None, ALU.mult)
 
         def change_direct(h, slots):
             for t in slots:
@@ -171,28 +196,28 @@ def tile_list_replay_inverse_dynamics_kernel(
                     h_slots[h][:, t, :],
                     direct[SUCCESSORS][h][t][:],
                     gains[:, DIRECT, t : t + 1],
-                    gained[h][t][:],
+                    gained[h][t],
                     ALU.mult,
                     ALU.subtract,
                 )
 
         def interleave(h, part):
             cols = slice(QUARTER * part, QUARTER * (part + 1))
-            nc.vector.tensor_copy(
-                h_bf[DIRECT][h][:, cols, :].rearrange("p (c e) t -> p c t e", e=4),
-                h_slots[h][:, :, cols].rearrange("p t (c e) -> p c t e", e=4),
+            nc.gpsimd.tensor_scalar(
+                h_bf[DIRECT][h][:, cols, :], h_slots[h][:, :, cols].rearrange("p t c -> p c t"), 1.0, 0.0, ALU.mult, ALU.add
             )
 
         def turn(i, j):
-            if i == STATES:
+            first = j not in difference
+            if first:
                 difference[j] = turn_banks.tile([P, PACK, P], F32, name="difference")
             for t in range(PACK):
                 nc.tensor.matmul(
                     difference[j][:, t, :],
                     turned[i][j][:, t, :],
                     ident[:],
-                    start=(i == STATES and t == 0),
-                    stop=(i == SUCCESSORS and t == PACK - 1),
+                    start=(first and t == 0),
+                    stop=(not first and t == PACK - 1),
                     is_transpose=True,
                 )
 
@@ -242,8 +267,8 @@ def tile_list_replay_inverse_dynamics_kernel(
         gather_scales(STATES)
         place_scales(STATES)
         load_w1(TURNED, on="staged_scales0")
-        nc.scalar.activation(*cast_views(DIRECT, 0), ACT.Copy)
-        nc.vector.tensor_copy(*cast_views(DIRECT, 1))
+        for u in range(2):
+            nc.scalar.activation(*cast_views(DIRECT, u), ACT.Copy)
         load_words(SUCCESSORS, tab2_words, on="w1_raw0")
         gather_scales(SUCCESSORS)
         quantize_w1(DIRECT)
@@ -252,63 +277,59 @@ def tile_list_replay_inverse_dynamics_kernel(
             gather_words(STATES, h)
             encode_direct(STATES, h, range(PACK))
         for u in range(2):
-            nc.vector.tensor_copy(*cast_views(TURNED, u))
+            cast_turned(u)
         quantize_w1(TURNED)
         load_w4()
         gain_states(0)
         gain_states(1)
-        for j in range(3):
+        for j in range(AHEAD):
             encode_turned(STATES, j)
         gather_words(SUCCESSORS, 0)
         gather_words(SUCCESSORS, 1)
-        for j in range(3):
+        for j in range(2):
             turn(STATES, j)
 
-        encode_direct(SUCCESSORS, 0, range(PACK))
-        change_direct(0, range(PACK))
-        for j in range(3):
-            encode_turned(SUCCESSORS, j)
-        encode_turned(STATES, 3)
-        encode_turned(SUCCESSORS, 3)
+        encode_direct(SUCCESSORS, 0, [0, 1])
+        encode_turned(SUCCESSORS, 0)
+        encode_direct(SUCCESSORS, 0, [2, 3])
+        encode_turned(SUCCESSORS, 1)
+        change_direct(0, [0, 1])
+        for j in (0, 1):
+            turn(SUCCESSORS, j)
+        change_direct(0, [2, 3])
         interleave(0, 0)
         interleave(0, 1)
-        for j in range(3):
-            turn(SUCCESSORS, j)
-        change_turned(0)
-        quantize_h(DIRECT, 0, 0, HALF)
-        change_turned(1)
-        change_turned(2)
-        encode_direct(SUCCESSORS, 1, [0, 1])
-        turn(STATES, 3)
-        turn(SUCCESSORS, 3)
-        change_turned(3)
-        encode_direct(SUCCESSORS, 1, [2, 3])
-        change_direct(1, [0])
+        encode_direct(SUCCESSORS, 1, range(PACK))
+        for j in (0, 1):
+            change_turned(j)
+        for i in (SUCCESSORS, STATES):
+            for j in (2, 3):
+                turn(i, j)
+        for j in (2, 3):
+            change_turned(j)
         quantize_h(TURNED, 0, 0, HALF)
-        change_direct(1, [1, 2, 3])
+        quantize_h(DIRECT, 0, 0, HALF)
 
-        for j in (4, 5):
-            encode_turned(STATES, j)
-            encode_turned(SUCCESSORS, j)
-        logits(0, 0, HALF, shared=False)
+        change_direct(1, range(PACK))
+        for pair in (2, 3):
+            encode_turned(STATES, pair)
         interleave(1, 0)
         interleave(1, 1)
-        for j in (4, 5):
+        for pair in (2, 3):
+            encode_turned(SUCCESSORS, pair)
+        for j in range(TILES, 2 * TILES):
             turn(STATES, j)
+        for j in range(TILES, 2 * TILES):
             turn(SUCCESSORS, j)
-        for j in (6, 7):
-            encode_turned(STATES, j)
-        for j in (6, 7):
-            encode_turned(SUCCESSORS, j)
+        logits(0, 0, HALF, shared=False)
         change_turned(4)
-        quantize_h(DIRECT, 1, 0, HALF)
         change_turned(5)
-        for i in (STATES, SUCCESSORS):
-            for j in (6, 7):
-                turn(i, j)
+        quantize_h(DIRECT, 1, 0, QUARTER)
         change_turned(6)
         quantize_h(TURNED, 1, 0, QUARTER)
+        quantize_h(DIRECT, 1, QUARTER, QUARTER)
+        quantize_h(TURNED, 1, QUARTER, P)
         change_turned(7)
-        logits(1, 0, QUARTER, shared=False)
-        quantize_h(TURNED, 1, QUARTER, QUARTER)
-        logits(1, QUARTER, QUARTER, shared=True)
+        logits(1, 0, HALF - P, shared=False)
+        quantize_h(TURNED, 1, QUARTER + P, P)
+        logits(1, HALF - P, P, shared=True)

@@ -51,8 +51,8 @@ def tile_list_replay_inverse_dynamics_kernel(
         lists = [keep.tile([P, S // STRIPE], U16, name=f"list{i}") for i in range(2)]
         staged_scales = [held(f"staged_scales{i}", [P, T // 4], I32) for i in range(2)]
         picked_rows = [held(f"picked_rows{i}", [P, S], U8) for i in range(2)]
-        gains = held("gains", [P, 2, PACK], F32)
-        biases = held("biases", [P, 2], F32)
+        gains, late = {}, {}
+        gain_rows = gain.rearrange("(g p t) -> g p t", g=2, t=PACK)
         ident = held("ident", [P, P], F32)
         table_words, w1_raw, picked_scales, w4 = {}, {}, {}, {}
         w1_rows = w1.rearrange("(p i) c -> p i c", i=PACK)
@@ -82,6 +82,15 @@ def tile_list_replay_inverse_dynamics_kernel(
                     picked_rows[i][rows.start + step * r : P : step * SCALE_ROWS, :].bitcast(I32),
                 )
 
+        def load_gain(g, queue, on=None):
+            gains[g] = held(f"gains{g}", [P, 1, PACK], F32, on)
+            queue.dma_start(gains[g][:, 0, :], gain_rows[g])
+
+        def load_bias(on):
+            late["biases"] = held("biases", [P, 2], F32, on)
+            with nc.allow_non_contiguous_dma(reason="one bias for each partition"):
+                nc.sync.dma_start(late["biases"][:], bias.rearrange("(c p) -> p c", p=P))
+
         def load_w4():
             w4["codes"] = held("w4_codes", [P, 2, N // 2], I32, "staged_scales0")
             w4["scale"] = held("w4_scale", [P, 2, N // 4], I32, "picked_rows1")
@@ -105,7 +114,6 @@ def tile_list_replay_inverse_dynamics_kernel(
         h_bf = [[held(f"h_bf{g}{h}", [P, HALF, PACK], BF16) for h in range(2)] for g in range(2)]
         h_codes = [[held(f"h_codes{g}{h}", [P, HALF], U32) for h in range(2)] for g in range(2)]
         h_scale = [[held(f"h_scale{g}{h}", [P, HALF], U8) for h in range(2)] for g in range(2)]
-        turned_gain = gains[:, TURNED : TURNED + 1, :].to_broadcast([P, P, PACK])
         out_rows = out.rearrange("(c p) j -> p c j", p=P)
 
         def scale_plane(i, first, count):
@@ -188,23 +196,24 @@ def tile_list_replay_inverse_dynamics_kernel(
                 for k in range(2):
                     gained[k] = [both[:, k, t, :] for t in range(PACK)]
             for t in range(PACK):
-                nc.vector.tensor_scalar(gained[h][t], direct[STATES][h][t][:], gains[:, DIRECT, t : t + 1], None, ALU.mult)
+                nc.vector.tensor_scalar(gained[h][t], direct[STATES][h][t][:], gains[DIRECT][:, 0, t : t + 1], None, ALU.mult)
 
         def change_direct(h, slots):
             for t in slots:
                 nc.vector.scalar_tensor_tensor(
                     h_slots[h][:, t, :],
                     direct[SUCCESSORS][h][t][:],
-                    gains[:, DIRECT, t : t + 1],
+                    gains[DIRECT][:, 0, t : t + 1],
                     gained[h][t],
                     ALU.mult,
                     ALU.subtract,
                 )
 
-        def interleave(h, part):
-            cols = slice(QUARTER * part, QUARTER * (part + 1))
-            nc.gpsimd.tensor_scalar(
-                h_bf[DIRECT][h][:, cols, :], h_slots[h][:, :, cols].rearrange("p t c -> p c t"), 1.0, 0.0, ALU.mult, ALU.add
+        def interleave(h, first, width):
+            cols = slice(first, first + width)
+            nc.vector.tensor_copy(
+                h_bf[DIRECT][h][:, cols, :].rearrange("p (c e) t -> p c t e", e=4),
+                h_slots[h][:, :, cols].rearrange("p t (c e) -> p c t e", e=4),
             )
 
         def turn(i, j):
@@ -224,7 +233,7 @@ def tile_list_replay_inverse_dynamics_kernel(
         def change_turned(j):
             cols = slice(P * (j % TILES), P * (j % TILES + 1))
             nc.vector.tensor_tensor(
-                h_bf[TURNED][j // TILES][:, cols, :], difference[j][:].rearrange("p t j -> p j t"), turned_gain, ALU.mult
+                h_bf[TURNED][j // TILES][:, cols, :], difference[j][:].rearrange("p t j -> p j t"), gains[TURNED][:].to_broadcast([P, P, PACK]), ALU.mult
             )
 
         def logits(h, first, width, shared):
@@ -246,9 +255,9 @@ def tile_list_replay_inverse_dynamics_kernel(
                             stop=(g == TURNED),
                         )
                 if shared and c == 1:
-                    nc.vector.tensor_scalar(result[:], acc[:], biases[:, c : c + 1], None, ALU.add)
+                    nc.vector.tensor_scalar(result[:], acc[:], late["biases"][:, c : c + 1], None, ALU.add)
                 else:
-                    nc.scalar.activation(result[:], acc[:], ACT.Identity, bias=biases[:, c : c + 1])
+                    nc.scalar.activation(result[:], acc[:], ACT.Identity, bias=late["biases"][:, c : c + 1])
                 nc.sync.dma_start(out_rows[:, c, tokens], result[:])
 
         nc.vector.memset(staged_scales[STATES][0 : STAGE_ROWS[STATES].start, :], 0)
@@ -259,9 +268,7 @@ def tile_list_replay_inverse_dynamics_kernel(
         load_w1(DIRECT)
         load_scales(SUCCESSORS, tab2_scales)
         load_words(STATES, tab_words)
-        nc.gpsimd.dma_start(gains[:], gain.rearrange("(g p t) -> p g t", g=2, t=PACK))
-        with nc.allow_non_contiguous_dma(reason="one bias for each partition"):
-            nc.gpsimd.dma_start(biases[:], bias.rearrange("(c p) -> p c", p=P))
+        load_gain(DIRECT, nc.gpsimd)
         make_identity(nc, ident[:])
 
         gather_scales(STATES)
@@ -279,7 +286,9 @@ def tile_list_replay_inverse_dynamics_kernel(
         for u in range(2):
             cast_turned(u)
         quantize_w1(TURNED)
+        load_gain(TURNED, nc.sync, on="staged_scales1")
         load_w4()
+        load_bias(on="table_words0")
         gain_states(0)
         gain_states(1)
         for j in range(AHEAD):
@@ -297,8 +306,7 @@ def tile_list_replay_inverse_dynamics_kernel(
         for j in (0, 1):
             turn(SUCCESSORS, j)
         change_direct(0, [2, 3])
-        interleave(0, 0)
-        interleave(0, 1)
+        interleave(0, 0, HALF)
         encode_direct(SUCCESSORS, 1, range(PACK))
         for j in (0, 1):
             change_turned(j)
@@ -313,8 +321,7 @@ def tile_list_replay_inverse_dynamics_kernel(
         change_direct(1, range(PACK))
         for pair in (2, 3):
             encode_turned(STATES, pair)
-        interleave(1, 0)
-        interleave(1, 1)
+        interleave(1, 0, HALF)
         for pair in (2, 3):
             encode_turned(SUCCESSORS, pair)
         for j in range(TILES, 2 * TILES):
@@ -324,10 +331,9 @@ def tile_list_replay_inverse_dynamics_kernel(
         logits(0, 0, HALF, shared=False)
         change_turned(4)
         change_turned(5)
-        quantize_h(DIRECT, 1, 0, QUARTER)
+        quantize_h(DIRECT, 1, 0, HALF)
         change_turned(6)
         quantize_h(TURNED, 1, 0, QUARTER)
-        quantize_h(DIRECT, 1, QUARTER, QUARTER)
         quantize_h(TURNED, 1, QUARTER, P)
         change_turned(7)
         logits(1, 0, HALF - P, shared=False)

@@ -32,7 +32,8 @@ STAGE_ROWS = (slice(112, 128), slice(4, 128, 8))
 SCALE_START = (0, 4)
 BANKS = 4
 TURNED_BUFS = 4
-AHEAD = 2
+WIDTH = (HALF, QUARTER)
+LATE = [(1, 2), (1, 3)]
 
 
 def tile_list_replay_inverse_dynamics_kernel(
@@ -106,11 +107,11 @@ def tile_list_replay_inverse_dynamics_kernel(
         w1_codes = [held(f"w1_codes{g}", [P, PASS], U32) for g in range(2)]
         w1_scale = [held(f"w1_scale{g}", [P, PASS], U8) for g in range(2)]
         picked_words = [[held(f"picked_words{i}{h}", [P, HALF], U32) for h in range(2)] for i in range(2)]
-        direct = [[[held(f"direct{i}{h}{t}", [P, HALF], F32) for t in range(PACK)] for h in range(2)] for i in range(2)]
+        direct = [[[held(f"direct{i}{h}{t}", [P, HALF], F32) for t in range(WIDTH[h] // P)] for h in range(2)] for i in range(2)]
         turned = [{}, {}]
         difference = {}
         gained = {}
-        h_slots = [held(f"h_slots{h}", [P, PACK, HALF], BF16) for h in range(2)]
+        h_slots = [held(f"h_slots{h}", [P, PACK, WIDTH[h]], BF16) for h in range(2)]
         h_bf = [[held(f"h_bf{g}{h}", [P, HALF, PACK], BF16) for h in range(2)] for g in range(2)]
         h_codes = [[held(f"h_codes{g}{h}", [P, HALF], U32) for h in range(2)] for g in range(2)]
         h_scale = [[held(f"h_scale{g}{h}", [P, HALF], U8) for h in range(2)] for g in range(2)]
@@ -143,67 +144,86 @@ def tile_list_replay_inverse_dynamics_kernel(
             cols = slice(first, first + width)
             quantize(h_codes[g][h][:, cols], h_scale[g][h][:, cols], h_bf[g][h][:, cols, :])
 
-        def encode_direct(i, h, slots):
-            for t in slots:
-                z = mx_banks.tile([P, HALF], F32, name="mx_out")
-                cols = slice(P * t, P * (t + 1))
-                nc.tensor.matmul_mx(
-                    out=z[:],
-                    lhsT=w1_codes[DIRECT][:, cols].bitcast(FP8X4),
-                    lhsT_scale=w1_scale[DIRECT][:, cols],
-                    rhs=picked_words[i][h][:].bitcast(FP8X4),
-                    rhs_scale=scale_plane(i, HALF * h, HALF),
-                    start=True,
-                    stop=True,
-                )
-                nc.scalar.activation(direct[i][h][t][:], z[:], ACT.Tanh)
+        def direct_slot(i, h, t):
+            first = WIDTH[h] * t
+            return direct[i][h][first // HALF][:, first % HALF : first % HALF + WIDTH[h]]
 
-        def encode_turned(i, pair):
-            if i == SUCCESSORS:
-                both = ring.tile([P, 2, PACK, P], F32, name="turned_successors")[:]
-            elif pair < AHEAD:
-                both = held(f"turned_states{pair}", [P, 2, PACK, P], F32)[:]
-            else:
-                if pair == AHEAD:
-                    w4["late"] = held("late_states", [P, TILES - AHEAD, 2, PACK, P], F32, "w1_raw0")
-                both = w4["late"][:, pair - AHEAD]
-            for e in range(2):
-                turned[i][2 * pair + e] = both[:, e]
-            for q in range(2):
-                cols = slice(PASS // 2 * q, PASS // 2 * (q + 1))
-                z = mx_banks.tile([P, 2, PASS // 2], F32, name="mx_out")
-                for e in range(2):
-                    j = 2 * pair + e
+        def encode_direct(i, h, banks):
+            width = WIDTH[h]
+            per_bank = HALF // width
+            for b in banks:
+                z = mx_banks.tile([P, per_bank, width], F32, name="mx_out")
+                for e in range(per_bank):
+                    t = per_bank * b + e
+                    cols = slice(P * t, P * (t + 1))
                     nc.tensor.matmul_mx(
                         out=z[:, e, :],
-                        lhsT=picked_words[i][j // TILES][:, P * (j % TILES) : P * (j % TILES + 1)].bitcast(FP8X4),
-                        lhsT_scale=scale_plane(i, P * j, P),
-                        rhs=w1_codes[TURNED][:, cols].bitcast(FP8X4),
-                        rhs_scale=w1_scale[TURNED][:, cols],
+                        lhsT=w1_codes[0][:, cols].bitcast(FP8X4),
+                        lhsT_scale=w1_scale[0][:, cols],
+                        rhs=picked_words[i][h][:, 0:width].bitcast(FP8X4),
+                        rhs_scale=scale_plane(i, HALF * h, width),
                         start=True,
                         stop=True,
                     )
-                nc.scalar.activation(
-                    both[:, :, :, P // 2 * q : P // 2 * (q + 1)],
-                    z[:].rearrange("p e (t m) -> p e t m", t=PACK),
-                    ACT.Tanh,
-                    scale=(-1.0 if i == STATES else 1.0),
-                )
+                nc.scalar.activation(direct[i][h][b][:], z[:].rearrange("p e j -> p (e j)"), ACT.Tanh)
+
+        def turned_product(i, g, j, cols, z):
+            nc.tensor.matmul_mx(
+                out=z,
+                lhsT=picked_words[i][j // TILES][:, P * (j % TILES) : P * (j % TILES + 1)].bitcast(FP8X4),
+                lhsT_scale=scale_plane(i, P * j, P),
+                rhs=w1_codes[g][:, cols].bitcast(FP8X4),
+                rhs_scale=w1_scale[g][:, cols],
+                start=True,
+                stop=True,
+            )
+
+        def encode_pair(i, g, pair):
+            if i == SUCCESSORS:
+                both = ring.tile([P, 2, PACK, P], F32, name="turned_successors")[:]
+            elif (g, pair) not in LATE:
+                both = held(f"turned_states{g}{pair}", [P, 2, PACK, P], F32)[:]
+            else:
+                if (g, pair) == LATE[0]:
+                    late["states"] = held("late_states", [P, len(LATE), 2, PACK, P], F32, "w1_raw0")
+                both = late["states"][:, LATE.index((g, pair))]
+            for e in range(2):
+                turned[i][g, 2 * pair + e] = both[:, e]
+            for q in range(2):
+                z = mx_banks.tile([P, 2, PASS // 2], F32, name="mx_out")
+                for e in range(2):
+                    turned_product(i, g, 2 * pair + e, slice(PASS // 2 * q, PASS // 2 * (q + 1)), z[:, e, :])
+                if g == 1:
+                    dst, src = both[:, :, :, P // 2 * q : P // 2 * (q + 1)], z[:].rearrange("p e (t m) -> p e t m", t=PACK)
+                else:
+                    dst, src = both[:, :, 2 * q : 2 * q + 2, :], z[:].rearrange("p e (t m) -> p e t m", t=2)
+                nc.scalar.activation(dst, src, ACT.Tanh, scale=(-1.0 if i == STATES else 1.0))
+
+        def encode_single(j):
+            turned[SUCCESSORS][1, j] = held(f"last_successors{j}", [P, PACK, P], F32)[:]
+            z = mx_banks.tile([P, PASS], F32, name="mx_out")
+            turned_product(SUCCESSORS, 1, j, slice(0, PASS), z[:])
+            nc.scalar.activation(
+                turned[SUCCESSORS][1, j].rearrange("p t (q m) -> p q t m", q=2),
+                z[:].rearrange("p (q t m) -> p q t m", q=2, t=PACK),
+                ACT.Tanh,
+            )
 
         def gain_states(h):
             if h == 0:
-                both = held("gained", [P, 2, PACK, HALF], F32, "w1_bf1")
+                both = held("gained", [P, PACK * sum(WIDTH)], F32, "w1_bf1")
                 for k in range(2):
-                    gained[k] = [both[:, k, t, :] for t in range(PACK)]
+                    first = PACK * WIDTH[0] * k
+                    gained[k] = [both[:, first + WIDTH[k] * t : first + WIDTH[k] * (t + 1)] for t in range(PACK)]
             for t in range(PACK):
-                nc.vector.tensor_scalar(gained[h][t], direct[STATES][h][t][:], gains[DIRECT][:, 0, t : t + 1], None, ALU.mult)
+                nc.vector.tensor_scalar(gained[h][t], direct_slot(STATES, h, t), gains[0][:, 0, t : t + 1], None, ALU.mult)
 
         def change_direct(h, slots):
             for t in slots:
                 nc.vector.scalar_tensor_tensor(
                     h_slots[h][:, t, :],
-                    direct[SUCCESSORS][h][t][:],
-                    gains[DIRECT][:, 0, t : t + 1],
+                    direct_slot(SUCCESSORS, h, t),
+                    gains[0][:, 0, t : t + 1],
                     gained[h][t],
                     ALU.mult,
                     ALU.subtract,
@@ -212,28 +232,35 @@ def tile_list_replay_inverse_dynamics_kernel(
         def interleave(h, first, width):
             cols = slice(first, first + width)
             nc.vector.tensor_copy(
-                h_bf[DIRECT][h][:, cols, :].rearrange("p (c e) t -> p c t e", e=4),
+                h_bf[0][h][:, cols, :].rearrange("p (c e) t -> p c t e", e=4),
                 h_slots[h][:, :, cols].rearrange("p t (c e) -> p c t e", e=4),
             )
 
-        def turn(i, j):
-            first = j not in difference
+        def interleave_on_scalar(h, first, width):
+            cols = slice(first, first + width)
+            nc.scalar.copy(h_bf[0][h][:, cols, :], h_slots[h][:, :, cols].rearrange("p t c -> p c t"))
+
+        def turn(i, g, j):
+            first = (g, j) not in difference
             if first:
-                difference[j] = turn_banks.tile([P, PACK, P], F32, name="difference")
+                difference[g, j] = turn_banks.tile([P, PACK, P], F32, name="difference")
             for t in range(PACK):
                 nc.tensor.matmul(
-                    difference[j][:, t, :],
-                    turned[i][j][:, t, :],
+                    difference[g, j][:, t, :],
+                    turned[i][g, j][:, t, :],
                     ident[:],
                     start=(first and t == 0),
                     stop=(not first and t == PACK - 1),
                     is_transpose=True,
                 )
 
-        def change_turned(j):
+        def change_turned(g, j):
             cols = slice(P * (j % TILES), P * (j % TILES + 1))
             nc.vector.tensor_tensor(
-                h_bf[TURNED][j // TILES][:, cols, :], difference[j][:].rearrange("p t j -> p j t"), gains[TURNED][:].to_broadcast([P, P, PACK]), ALU.mult
+                h_bf[g][j // TILES][:, cols, :],
+                difference[g, j][:].rearrange("p t j -> p j t"),
+                gains[g][:].to_broadcast([P, P, PACK]),
+                ALU.mult,
             )
 
         def logits(h, first, width, shared):
@@ -282,60 +309,67 @@ def tile_list_replay_inverse_dynamics_kernel(
         place_scales(SUCCESSORS, on="w1_bf0")
         for h in range(2):
             gather_words(STATES, h)
-            encode_direct(STATES, h, range(PACK))
+            encode_direct(STATES, h, range(WIDTH[h] // P))
         for u in range(2):
             cast_turned(u)
         quantize_w1(TURNED)
-        load_gain(TURNED, nc.sync, on="staged_scales1")
+        load_gain(TURNED, nc.sync, on="picked_rows0")
         load_w4()
         load_bias(on="table_words0")
         gain_states(0)
         gain_states(1)
-        for j in range(AHEAD):
-            encode_turned(STATES, j)
+        for g, pair in ((1, 0), (1, 1), (0, 3)):
+            encode_pair(STATES, g, pair)
         gather_words(SUCCESSORS, 0)
         gather_words(SUCCESSORS, 1)
-        for j in range(2):
-            turn(STATES, j)
+        for j in range(TILES):
+            turn(STATES, 1, j)
 
         encode_direct(SUCCESSORS, 0, [0, 1])
-        encode_turned(SUCCESSORS, 0)
+        encode_pair(SUCCESSORS, 1, 0)
         encode_direct(SUCCESSORS, 0, [2, 3])
-        encode_turned(SUCCESSORS, 1)
+        encode_pair(SUCCESSORS, 1, 1)
         change_direct(0, [0, 1])
         for j in (0, 1):
-            turn(SUCCESSORS, j)
+            turn(SUCCESSORS, 1, j)
         change_direct(0, [2, 3])
-        interleave(0, 0, HALF)
-        encode_direct(SUCCESSORS, 1, range(PACK))
+        encode_direct(SUCCESSORS, 1, range(2))
         for j in (0, 1):
-            change_turned(j)
-        for i in (SUCCESSORS, STATES):
-            for j in (2, 3):
-                turn(i, j)
+            change_turned(1, j)
+        interleave(0, 0, HALF)
         for j in (2, 3):
-            change_turned(j)
-        quantize_h(TURNED, 0, 0, HALF)
-        quantize_h(DIRECT, 0, 0, HALF)
+            turn(SUCCESSORS, 1, j)
+        for j in (2, 3):
+            change_turned(1, j)
+        encode_pair(SUCCESSORS, 0, 3)
+        change_direct(1, [0])
+        quantize_h(1, 0, 0, HALF)
 
-        change_direct(1, range(PACK))
+        change_direct(1, [1, 2, 3])
+        quantize_h(0, 0, 0, HALF)
         for pair in (2, 3):
-            encode_turned(STATES, pair)
-        interleave(1, 0, HALF)
-        for pair in (2, 3):
-            encode_turned(SUCCESSORS, pair)
+            encode_pair(STATES, 1, pair)
+        encode_pair(SUCCESSORS, 1, 2)
+        interleave(1, 0, QUARTER)
+        for i in (SUCCESSORS, STATES):
+            for j in (6, 7):
+                turn(i, 0, j)
+        for j in (6, 7):
+            change_turned(0, j)
+        for j in (6, 7):
+            encode_single(j)
         for j in range(TILES, 2 * TILES):
-            turn(STATES, j)
+            turn(STATES, 1, j)
         for j in range(TILES, 2 * TILES):
-            turn(SUCCESSORS, j)
+            turn(SUCCESSORS, 1, j)
         logits(0, 0, HALF, shared=False)
-        change_turned(4)
-        change_turned(5)
-        quantize_h(DIRECT, 1, 0, HALF)
-        change_turned(6)
-        quantize_h(TURNED, 1, 0, QUARTER)
-        quantize_h(TURNED, 1, QUARTER, P)
-        change_turned(7)
-        logits(1, 0, HALF - P, shared=False)
-        quantize_h(TURNED, 1, QUARTER + P, P)
-        logits(1, HALF - P, P, shared=True)
+        quantize_h(0, 1, 0, HALF)
+        change_turned(1, 4)
+        change_turned(1, 5)
+        change_turned(1, 6)
+        quantize_h(1, 1, 0, QUARTER)
+        change_turned(1, 7)
+        quantize_h(1, 1, QUARTER, P)
+        quantize_h(1, 1, QUARTER + P, P)
+        logits(1, 0, QUARTER, shared=False)
+        logits(1, QUARTER, QUARTER, shared=True)

@@ -325,23 +325,23 @@ def tile_list_replay_inverse_dynamics_kernel(
         for j in range(TILES):
             turn(STATES, 1, j)
 
-        encode_direct(SUCCESSORS, 0, [0, 1])
+        encode_direct(SUCCESSORS, 0, range(PACK))
+        change_direct(0, range(PACK))
         encode_pair(SUCCESSORS, 1, 0)
-        encode_direct(SUCCESSORS, 0, [2, 3])
         encode_pair(SUCCESSORS, 1, 1)
-        change_direct(0, [0, 1])
+        interleave(0, 0, HALF)
         for j in (0, 1):
             turn(SUCCESSORS, 1, j)
-        change_direct(0, [2, 3])
         encode_direct(SUCCESSORS, 1, range(2))
         for j in (0, 1):
             change_turned(1, j)
-        interleave(0, 0, HALF)
         for j in (2, 3):
             turn(SUCCESSORS, 1, j)
         for j in (2, 3):
             change_turned(1, j)
         encode_pair(SUCCESSORS, 0, 3)
+        for j in (6, 7):
+            turn(STATES, 0, j)
         change_direct(1, [0])
         quantize_h(1, 0, 0, HALF)
 
@@ -351,9 +351,8 @@ def tile_list_replay_inverse_dynamics_kernel(
             encode_pair(STATES, 1, pair)
         encode_pair(SUCCESSORS, 1, 2)
         interleave(1, 0, QUARTER)
-        for i in (SUCCESSORS, STATES):
-            for j in (6, 7):
-                turn(i, 0, j)
+        for j in (6, 7):
+            turn(SUCCESSORS, 0, j)
         for j in (6, 7):
             change_turned(0, j)
         for j in (6, 7):

@@ -43,8 +43,12 @@ def tile_list_replay_inverse_dynamics_kernel(
     with ExitStack() as ctx:
         keep = ctx.enter_context(tc.tile_pool(name="keep", bufs=1))
         ring = ctx.enter_context(tc.tile_pool(name="ring", bufs=TURNED_BUFS))
-        mx_banks = ctx.enter_context(tc.psum_pool(name="mx_banks", bufs=BANKS))
-        turn_banks = ctx.enter_context(tc.psum_pool(name="turn_banks", bufs=BANKS))
+        psum = ctx.enter_context(tc.psum_pool(name="psum", bufs=1))
+        taken = {"mx": 0, "turn": 0}
+
+        def bank(kind, shape):
+            taken[kind] = taken[kind] + 1
+            return psum.tile(shape, F32, name=f"{kind}{taken[kind]}", tag=f"{kind}_bank{taken[kind] % BANKS}")
 
         def held(name, shape, dtype, on=None):
             return keep.tile(shape, dtype, name=name, tag=on or name, align_bytes=64)
@@ -152,7 +156,7 @@ def tile_list_replay_inverse_dynamics_kernel(
             width = WIDTH[h]
             per_bank = HALF // width
             for b in banks:
-                z = mx_banks.tile([P, per_bank, width], F32, name="mx_out")
+                z = bank("mx", [P, per_bank, width])
                 for e in range(per_bank):
                     t = per_bank * b + e
                     cols = slice(P * t, P * (t + 1))
@@ -190,7 +194,7 @@ def tile_list_replay_inverse_dynamics_kernel(
             for e in range(2):
                 turned[i][g, 2 * pair + e] = both[:, e]
             for q in range(2):
-                z = mx_banks.tile([P, 2, PASS // 2], F32, name="mx_out")
+                z = bank("mx", [P, 2, PASS // 2])
                 for e in range(2):
                     turned_product(i, g, 2 * pair + e, slice(PASS // 2 * q, PASS // 2 * (q + 1)), z[:, e, :])
                 if g == 1:
@@ -201,7 +205,7 @@ def tile_list_replay_inverse_dynamics_kernel(
 
         def encode_single(j):
             turned[SUCCESSORS][1, j] = held(f"last_successors{j}", [P, PACK, P], F32)[:]
-            z = mx_banks.tile([P, PASS], F32, name="mx_out")
+            z = bank("mx", [P, PASS])
             turned_product(SUCCESSORS, 1, j, slice(0, PASS), z[:])
             nc.scalar.activation(
                 turned[SUCCESSORS][1, j].rearrange("p t (q m) -> p q t m", q=2),
@@ -243,11 +247,11 @@ def tile_list_replay_inverse_dynamics_kernel(
         def turn(i, g, j):
             first = (g, j) not in difference
             if first:
-                difference[g, j] = turn_banks.tile([P, PACK, P], F32, name="difference")
+                difference[g, j] = bank("turn", [P, PACK, P])
             for t in range(PACK):
                 nc.tensor.matmul(
-                    difference[g, j][:, t, :],
-                    turned[i][g, j][:, t, :],
+                    difference[g, j][:, PACK - 1 - t, :],
+                    turned[i][g, j][:, PACK - 1 - t, :],
                     ident[:],
                     start=(first and t == 0),
                     stop=(not first and t == PACK - 1),
@@ -268,7 +272,7 @@ def tile_list_replay_inverse_dynamics_kernel(
             step = HALF if width == HALF else P
             for c in range(2):
                 result = held(f"result{h}_{first}_{c}", [P, width], F32)
-                acc = mx_banks.tile([P, width], F32, name="mx_out")
+                acc = bank("mx", [P, width])
                 for n0 in range(0, width, step):
                     cols = slice(first + n0, first + n0 + step)
                     for g in (DIRECT, TURNED):
@@ -330,43 +334,45 @@ def tile_list_replay_inverse_dynamics_kernel(
         encode_pair(SUCCESSORS, 1, 0)
         encode_pair(SUCCESSORS, 1, 1)
         interleave(0, 0, HALF)
-        for j in (0, 1):
-            turn(SUCCESSORS, 1, j)
         encode_direct(SUCCESSORS, 1, range(2))
         for j in (0, 1):
+            turn(SUCCESSORS, 1, j)
+        for j in (0, 1):
             change_turned(1, j)
+        encode_pair(SUCCESSORS, 0, 3)
         for j in (2, 3):
             turn(SUCCESSORS, 1, j)
         for j in (2, 3):
             change_turned(1, j)
-        encode_pair(SUCCESSORS, 0, 3)
-        for j in (6, 7):
-            turn(STATES, 0, j)
         change_direct(1, [0])
         quantize_h(1, 0, 0, HALF)
 
         change_direct(1, [1, 2, 3])
         quantize_h(0, 0, 0, HALF)
-        for pair in (2, 3):
-            encode_pair(STATES, 1, pair)
+        encode_pair(STATES, 1, 2)
         encode_pair(SUCCESSORS, 1, 2)
         interleave(1, 0, QUARTER)
         for j in (6, 7):
             turn(SUCCESSORS, 0, j)
+            turn(STATES, 0, j)
         for j in (6, 7):
             change_turned(0, j)
+        encode_pair(STATES, 1, 3)
         for j in (6, 7):
             encode_single(j)
-        for j in range(TILES, 2 * TILES):
+        for j in (4, 5):
+            turn(SUCCESSORS, 1, j)
             turn(STATES, 1, j)
-        for j in range(TILES, 2 * TILES):
+        for j in (6, 7):
+            turn(STATES, 1, j)
+        for j in (6, 7):
             turn(SUCCESSORS, 1, j)
         logits(0, 0, HALF, shared=False)
         quantize_h(0, 1, 0, HALF)
         change_turned(1, 4)
         change_turned(1, 5)
-        change_turned(1, 6)
         quantize_h(1, 1, 0, QUARTER)
+        change_turned(1, 6)
         change_turned(1, 7)
         quantize_h(1, 1, QUARTER, P)
         quantize_h(1, 1, QUARTER + P, P)

@@ -28,7 +28,7 @@ QUADRANT = 32
 SCALE_ROWS = 4
 STATES, SUCCESSORS = 0, 1
 DIRECT, TURNED = 0, 1
-STAGE_ROWS = (slice(112, 128), slice(4, 128, 8))
+STAGE_ROWS = (slice(112, 128), slice(32, 96, 4))
 SCALE_START = (0, 4)
 BANKS = 4
 TURNED_BUFS = 4
@@ -78,13 +78,13 @@ def tile_list_replay_inverse_dynamics_kernel(
 
         def place_scales(i, on=None):
             picked_scales[i] = held(f"picked_scales{i}", [P, S // 4], I32, on)
-            nc.vector.memset(picked_scales[i][:], 0)
+            (nc.gpsimd if on else nc.vector).memset(picked_scales[i][:], 0)
             rows = STAGE_ROWS[i]
             step = rows.step or 1
             for r in range(SCALE_ROWS):
                 nc.sync.dma_start(
                     picked_scales[i][SCALE_START[i] + r : P : QUADRANT, :],
-                    picked_rows[i][rows.start + step * r : P : step * SCALE_ROWS, :].bitcast(I32),
+                    picked_rows[i][rows.start + step * r : rows.stop : step * SCALE_ROWS, :].bitcast(I32),
                 )
 
         def load_gain(g, queue, on=None):
@@ -99,7 +99,7 @@ def tile_list_replay_inverse_dynamics_kernel(
         def load_w4():
             w4["codes"] = held("w4_codes", [P, 2, N // 2], I32, "staged_scales0")
             w4["scale"] = held("w4_scale", [P, 2, N // 4], I32, "picked_rows1")
-            nc.vector.memset(w4["scale"][:], 0)
+            nc.gpsimd.memset(w4["scale"][:], 0)
             nc.sync.dma_start(w4["codes"][:], w4_words.bitcast(I32).rearrange("g p c -> p g c"))
             for r in range(SCALE_ROWS):
                 nc.sync.dma_start(
@@ -113,7 +113,7 @@ def tile_list_replay_inverse_dynamics_kernel(
         picked_words = [[held(f"picked_words{i}{h}", [P, HALF], U32) for h in range(2)] for i in range(2)]
         direct = [[[held(f"direct{i}{h}{t}", [P, HALF], F32) for t in range(WIDTH[h] // P)] for h in range(2)] for i in range(2)]
         turned = [{}, {}]
-        difference = {}
+        difference, sums = {}, {}
         gained = {}
         h_slots = [held(f"h_slots{h}", [P, PACK, WIDTH[h]], BF16) for h in range(2)]
         h_bf = [[held(f"h_bf{g}{h}", [P, HALF, PACK], BF16) for h in range(2)] for g in range(2)]
@@ -267,12 +267,11 @@ def tile_list_replay_inverse_dynamics_kernel(
                 ALU.mult,
             )
 
-        def logits(h, first, width, shared):
-            tokens = slice(HALF * h + first, HALF * h + first + width)
+        def logit_products(h, first, width, rows=(0, 1)):
             step = HALF if width == HALF else P
-            for c in range(2):
-                result = held(f"result{h}_{first}_{c}", [P, width], F32)
+            for c in rows:
                 acc = bank("mx", [P, width])
+                sums[h, first, c] = acc
                 for n0 in range(0, width, step):
                     cols = slice(first + n0, first + n0 + step)
                     for g in (DIRECT, TURNED):
@@ -285,6 +284,12 @@ def tile_list_replay_inverse_dynamics_kernel(
                             start=(g == DIRECT),
                             stop=(g == TURNED),
                         )
+
+        def store_logits(h, first, width, shared):
+            tokens = slice(HALF * h + first, HALF * h + first + width)
+            for c in range(2):
+                result = held(f"result{h}_{first}_{c}", [P, width], F32)
+                acc = sums[h, first, c]
                 if shared and c == 1:
                     nc.vector.tensor_scalar(result[:], acc[:], late["biases"][:, c : c + 1], None, ALU.add)
                 else:
@@ -358,16 +363,19 @@ def tile_list_replay_inverse_dynamics_kernel(
         for j in (6, 7):
             change_turned(0, j)
         encode_pair(STATES, 1, 3)
+        for j in (4, 5):
+            turn(STATES, 1, j)
         for j in (6, 7):
             encode_single(j)
         for j in (4, 5):
             turn(SUCCESSORS, 1, j)
-            turn(STATES, 1, j)
+        logit_products(0, 0, HALF, rows=(0,))
         for j in (6, 7):
             turn(STATES, 1, j)
         for j in (6, 7):
             turn(SUCCESSORS, 1, j)
-        logits(0, 0, HALF, shared=False)
+        logit_products(0, 0, HALF, rows=(1,))
+        store_logits(0, 0, HALF, shared=False)
         quantize_h(0, 1, 0, HALF)
         change_turned(1, 4)
         change_turned(1, 5)
@@ -376,5 +384,6 @@ def tile_list_replay_inverse_dynamics_kernel(
         change_turned(1, 7)
         quantize_h(1, 1, QUARTER, P)
         quantize_h(1, 1, QUARTER + P, P)
-        logits(1, 0, QUARTER, shared=False)
-        logits(1, QUARTER, QUARTER, shared=True)
+        for first in (0, QUARTER):
+            logit_products(1, first, QUARTER)
+            store_logits(1, first, QUARTER, shared=(first > 0))

@@ -33,6 +33,7 @@ SCALE_START = (0, 4)
 BANKS = 4
 TURNED_BUFS = 4
 WIDTH = (HALF, QUARTER)
+DIRECT_FIRST = (0, QUARTER)
 LATE = [(1, 2), (1, 3)]
 
 
@@ -78,7 +79,7 @@ def tile_list_replay_inverse_dynamics_kernel(
 
         def place_scales(i, on=None):
             picked_scales[i] = held(f"picked_scales{i}", [P, S // 4], I32, on)
-            (nc.gpsimd if on else nc.vector).memset(picked_scales[i][:], 0)
+            nc.vector.memset(picked_scales[i][:], 0)
             rows = STAGE_ROWS[i]
             step = rows.step or 1
             for r in range(SCALE_ROWS):
@@ -164,8 +165,8 @@ def tile_list_replay_inverse_dynamics_kernel(
                         out=z[:, e, :],
                         lhsT=w1_codes[0][:, cols].bitcast(FP8X4),
                         lhsT_scale=w1_scale[0][:, cols],
-                        rhs=picked_words[i][h][:, 0:width].bitcast(FP8X4),
-                        rhs_scale=scale_plane(i, HALF * h, width),
+                        rhs=picked_words[i][h][:, DIRECT_FIRST[h] : DIRECT_FIRST[h] + width].bitcast(FP8X4),
+                        rhs_scale=scale_plane(i, HALF * h + DIRECT_FIRST[h], width),
                         start=True,
                         stop=True,
                     )
@@ -240,9 +241,12 @@ def tile_list_replay_inverse_dynamics_kernel(
                 h_slots[h][:, :, cols].rearrange("p t (c e) -> p c t e", e=4),
             )
 
-        def interleave_on_scalar(h, first, width):
-            cols = slice(first, first + width)
-            nc.scalar.copy(h_bf[0][h][:, cols, :], h_slots[h][:, :, cols].rearrange("p t c -> p c t"))
+        def interleave_on_scalar(h):
+            late["quarter"] = held("late_quarter", [P, QUARTER, PACK], BF16, "picked_words11")
+            nc.scalar.copy(
+                late["quarter"][:].rearrange("p (c e) t -> p c t e", e=4),
+                h_slots[h][:].rearrange("p t (c e) -> p c t e", e=4),
+            )
 
         def turn(i, g, j):
             first = (g, j) not in difference
@@ -270,7 +274,7 @@ def tile_list_replay_inverse_dynamics_kernel(
         def logit_products(h, first, width, rows=(0, 1)):
             step = HALF if width == HALF else P
             for c in rows:
-                acc = bank("mx", [P, width])
+                acc = bank("turn" if first else "mx", [P, width])
                 sums[h, first, c] = acc
                 for n0 in range(0, width, step):
                     cols = slice(first + n0, first + n0 + step)
@@ -327,7 +331,7 @@ def tile_list_replay_inverse_dynamics_kernel(
         load_bias(on="table_words0")
         gain_states(0)
         gain_states(1)
-        for g, pair in ((1, 0), (1, 1), (0, 3)):
+        for g, pair in ((1, 0), (1, 1), (0, 2)):
             encode_pair(STATES, g, pair)
         gather_words(SUCCESSORS, 0)
         gather_words(SUCCESSORS, 1)
@@ -339,16 +343,18 @@ def tile_list_replay_inverse_dynamics_kernel(
         encode_pair(SUCCESSORS, 1, 0)
         encode_pair(SUCCESSORS, 1, 1)
         interleave(0, 0, HALF)
+        for j in (0, 1):
+            turn(SUCCESSORS, 1, j)
         encode_direct(SUCCESSORS, 1, range(2))
         for j in (0, 1):
-            turn(SUCCESSORS, 1, j)
-        for j in (0, 1):
             change_turned(1, j)
-        encode_pair(SUCCESSORS, 0, 3)
         for j in (2, 3):
             turn(SUCCESSORS, 1, j)
         for j in (2, 3):
             change_turned(1, j)
+        encode_pair(SUCCESSORS, 0, 2)
+        for j in (4, 5):
+            turn(STATES, 0, j)
         change_direct(1, [0])
         quantize_h(1, 0, 0, HALF)
 
@@ -356,17 +362,16 @@ def tile_list_replay_inverse_dynamics_kernel(
         quantize_h(0, 0, 0, HALF)
         encode_pair(STATES, 1, 2)
         encode_pair(SUCCESSORS, 1, 2)
-        interleave(1, 0, QUARTER)
-        for j in (6, 7):
+        for j in (4, 5):
             turn(SUCCESSORS, 0, j)
-            turn(STATES, 0, j)
-        for j in (6, 7):
+        for j in (4, 5):
             change_turned(0, j)
         encode_pair(STATES, 1, 3)
         for j in (4, 5):
             turn(STATES, 1, j)
         for j in (6, 7):
             encode_single(j)
+        interleave_on_scalar(1)
         for j in (4, 5):
             turn(SUCCESSORS, 1, j)
         logit_products(0, 0, HALF, rows=(0,))
@@ -376,12 +381,13 @@ def tile_list_replay_inverse_dynamics_kernel(
             turn(SUCCESSORS, 1, j)
         logit_products(0, 0, HALF, rows=(1,))
         store_logits(0, 0, HALF, shared=False)
-        quantize_h(0, 1, 0, HALF)
         change_turned(1, 4)
+        quantize_h(0, 1, 0, QUARTER)
         change_turned(1, 5)
         quantize_h(1, 1, 0, QUARTER)
         change_turned(1, 6)
         change_turned(1, 7)
+        quantize(h_codes[0][1][:, QUARTER:HALF], h_scale[0][1][:, QUARTER:HALF], late["quarter"][:])
         quantize_h(1, 1, QUARTER, P)
         quantize_h(1, 1, QUARTER + P, P)
         for first in (0, QUARTER):

@@ -20,6 +20,7 @@ ALU = mybir.AluOpType
 P = 128
 PACK = 4
 PASS = P * PACK
+PIECE = PASS // 2
 HALF = S // 2
 QUARTER = S // 4
 TILES = HALF // P
@@ -27,14 +28,13 @@ STRIPE = 16
 QUADRANT = 32
 SCALE_ROWS = 4
 STATES, SUCCESSORS = 0, 1
-DIRECT, TURNED = 0, 1
+EARLY, LATE = 0, 1
 STAGE_ROWS = (slice(112, 128), slice(32, 96, 4))
 SCALE_START = (0, 4)
 BANKS = 4
-TURNED_BUFS = 4
-WIDTH = (HALF, QUARTER)
-DIRECT_FIRST = (0, QUARTER)
-LATE = [(1, 2), (1, 3)]
+GROUPS = ((0, HALF), (HALF, QUARTER), (HALF + QUARTER, QUARTER))
+FRONT, MIDDLE, BACK = 0, 1, 2
+DIRECT_PASS = {FRONT: EARLY, BACK: LATE}
 
 
 def tile_list_replay_inverse_dynamics_kernel(
@@ -43,7 +43,6 @@ def tile_list_replay_inverse_dynamics_kernel(
     nc = tc.nc
     with ExitStack() as ctx:
         keep = ctx.enter_context(tc.tile_pool(name="keep", bufs=1))
-        ring = ctx.enter_context(tc.tile_pool(name="ring", bufs=TURNED_BUFS))
         psum = ctx.enter_context(tc.psum_pool(name="psum", bufs=1))
         taken = {"mx": 0, "turn": 0}
 
@@ -57,10 +56,10 @@ def tile_list_replay_inverse_dynamics_kernel(
         lists = [keep.tile([P, S // STRIPE], U16, name=f"list{i}") for i in range(2)]
         staged_scales = [held(f"staged_scales{i}", [P, T // 4], I32) for i in range(2)]
         picked_rows = [held(f"picked_rows{i}", [P, S], U8) for i in range(2)]
-        gains, late = {}, {}
-        gain_rows = gain.rearrange("(g p t) -> g p t", g=2, t=PACK)
+        picked_scales = {}
+        gains = held("gains", [P, 2, PACK], F32)
         ident = held("ident", [P, P], F32)
-        table_words, w1_raw, picked_scales, w4 = {}, {}, {}, {}
+        table_words, raw, late = {}, {}, {}
         w1_rows = w1.rearrange("(p i) c -> p i c", i=PACK)
 
         def load_words(i, src, on=None):
@@ -68,8 +67,8 @@ def tile_list_replay_inverse_dynamics_kernel(
             nc.sync.dma_start(table_words[i][:], src[0].rearrange("p t i -> p (t i)").bitcast(I32))
 
         def load_w1(g, on=None):
-            w1_raw[g] = held(f"w1_raw{g}", [P, PACK, PASS], F32, on)
-            nc.sync.dma_start(w1_raw[g][:], w1_rows[:, :, PASS * g : PASS * (g + 1)])
+            raw[g] = held(f"w1_raw{g}", [P, PACK, PASS], F32, on)
+            nc.sync.dma_start(raw[g][:], w1_rows[:, :, PASS * g : PASS * (g + 1)])
 
         def load_scales(i, src):
             nc.sync.dma_start(staged_scales[i][STAGE_ROWS[i], :], src[0].bitcast(I32))
@@ -88,174 +87,158 @@ def tile_list_replay_inverse_dynamics_kernel(
                     picked_rows[i][rows.start + step * r : rows.stop : step * SCALE_ROWS, :].bitcast(I32),
                 )
 
-        def load_gain(g, queue, on=None):
-            gains[g] = held(f"gains{g}", [P, 1, PACK], F32, on)
-            queue.dma_start(gains[g][:, 0, :], gain_rows[g])
-
-        def load_bias(on):
-            late["biases"] = held("biases", [P, 2], F32, on)
+        def load_rest():
+            late["w4_scale"] = held("w4_scale", [P, 2, N // 4], I32, "picked_rows1")
+            nc.gpsimd.memset(late["w4_scale"][:], 0)
+            late["w4_codes"] = held("w4_codes", [P, 2, N // 2], I32, "staged_scales0")
+            nc.sync.dma_start(late["w4_codes"][:], w4_words.bitcast(I32).rearrange("g p c -> p g c"))
+            for r in range(SCALE_ROWS):
+                nc.sync.dma_start(
+                    late["w4_scale"][r:P:QUADRANT, :, :],
+                    w4_scales.bitcast(I32)[:, r::SCALE_ROWS, :].rearrange("g q c -> q g c"),
+                )
+            late["biases"] = held("biases", [P, 2], F32, "table_words0")
             with nc.allow_non_contiguous_dma(reason="one bias for each partition"):
                 nc.sync.dma_start(late["biases"][:], bias.rearrange("(c p) -> p c", p=P))
 
-        def load_w4():
-            w4["codes"] = held("w4_codes", [P, 2, N // 2], I32, "staged_scales0")
-            w4["scale"] = held("w4_scale", [P, 2, N // 4], I32, "picked_rows1")
-            nc.gpsimd.memset(w4["scale"][:], 0)
-            nc.sync.dma_start(w4["codes"][:], w4_words.bitcast(I32).rearrange("g p c -> p g c"))
-            for r in range(SCALE_ROWS):
-                nc.sync.dma_start(
-                    w4["scale"][r:P:QUADRANT, :, :],
-                    w4_scales.bitcast(I32)[:, r::SCALE_ROWS, :].rearrange("g q c -> q g c"),
-                )
-
-        w1_bf = [held(f"w1_bf{g}", [P, PASS, PACK], BF16) for g in range(2)]
+        w1_bf = [[held(f"w1_bf{g}{u}", [P, PIECE, PACK], BF16) for u in range(2)] for g in range(2)]
         w1_codes = [held(f"w1_codes{g}", [P, PASS], U32) for g in range(2)]
         w1_scale = [held(f"w1_scale{g}", [P, PASS], U8) for g in range(2)]
         picked_words = [[held(f"picked_words{i}{h}", [P, HALF], U32) for h in range(2)] for i in range(2)]
-        direct = [[[held(f"direct{i}{h}{t}", [P, HALF], F32) for t in range(WIDTH[h] // P)] for h in range(2)] for i in range(2)]
-        turned = [{}, {}]
-        difference, sums = {}, {}
-        gained = {}
-        h_slots = [held(f"h_slots{h}", [P, PACK, WIDTH[h]], BF16) for h in range(2)]
-        h_bf = [[held(f"h_bf{g}{h}", [P, HALF, PACK], BF16) for h in range(2)] for g in range(2)]
-        h_codes = [[held(f"h_codes{g}{h}", [P, HALF], U32) for h in range(2)] for g in range(2)]
-        h_scale = [[held(f"h_scale{g}{h}", [P, HALF], U8) for h in range(2)] for g in range(2)]
+        direct, gained, turned, difference, sums = {}, {}, {}, {}, {}
+        h_slots = {BACK: held("h_slots_back", [P, PACK, QUARTER], BF16)}
+        h_bf = [[held(f"h_bf{g}{k}", [P, GROUPS[k][1], PACK], BF16) for k in range(3 - g)] + [None] * g for g in range(2)]
+        h_codes = [[held(f"h_codes{g}{k}", [P, GROUPS[k][1]], U32) for k in range(3)] for g in range(2)]
+        h_scale = [[held(f"h_scale{g}{k}", [P, GROUPS[k][1]], U8) for k in range(3)] for g in range(2)]
         out_rows = out.rearrange("(c p) j -> p c j", p=P)
 
-        def scale_plane(i, first, count):
-            return picked_scales[i][SCALE_START[i] : P, :].bitcast(U8)[:, first : first + count]
+        def tokens(i, first, count):
+            words = picked_words[i][first // HALF][:, first % HALF : first % HALF + count].bitcast(FP8X4)
+            return words, picked_scales[i][SCALE_START[i] : P, :].bitcast(U8)[:, first : first + count]
 
         def gather_words(i, h):
             offsets = lists[i][:, HALF * h // STRIPE : HALF * (h + 1) // STRIPE]
             nc.vector.tensor_copy(picked_words[i][h][:], table_words[i][:].bitcast(U32).indirect(offsets))
 
         def cast_views(g, u):
-            dst = w1_bf[g][:].rearrange("p (u e m) i -> p u m e i", u=2, e=2)
-            src = w1_raw[g][:].rearrange("p i (m u e) -> p u m e i", u=2, e=2)
-            return dst[:, u], src[:, u]
-
-        def cast_turned(u):
-            dst = w1_bf[TURNED][:].rearrange("p (q u e m) i -> p u q m e i", q=2, u=2, e=2)
-            src = w1_raw[TURNED][:].rearrange("p i (q m u e) -> p u q m e i", q=2, u=2, e=2)
-            nc.vector.tensor_copy(dst[:, u], src[:, u])
+            dst = w1_bf[g][u][:].rearrange("p (e m) i -> p m e i", e=2)
+            return dst, raw[g][:].rearrange("p i (m u e) -> p u m e i", u=2, e=2)[:, u]
 
         def quantize(codes, scale, src):
             nc.vector.quantize_mx(out=codes.bitcast(FP8X4), scales=scale, in_=src.rearrange("p c i -> p (c i)"))
 
-        def quantize_w1(g):
-            quantize(w1_codes[g][:], w1_scale[g][:], w1_bf[g][:])
+        def quantize_w1(g, u):
+            cols = slice(PIECE * u, PIECE * (u + 1))
+            quantize(w1_codes[g][:, cols], w1_scale[g][:, cols], w1_bf[g][u][:])
 
-        def quantize_h(g, h, first, width):
-            cols = slice(first, first + width)
-            quantize(h_codes[g][h][:, cols], h_scale[g][h][:, cols], h_bf[g][h][:, cols, :])
+        def quantize_h(g, k, first=0, width=None):
+            cols = slice(first, first + (width or GROUPS[k][1]))
+            quantize(h_codes[g][k][:, cols], h_scale[g][k][:, cols], h_bf[g][k][:, cols, :])
 
-        def direct_slot(i, h, t):
-            first = WIDTH[h] * t
-            return direct[i][h][first // HALF][:, first % HALF : first % HALF + WIDTH[h]]
-
-        def encode_direct(i, h, banks):
-            width = WIDTH[h]
-            per_bank = HALF // width
-            for b in banks:
-                z = bank("mx", [P, per_bank, width])
-                for e in range(per_bank):
-                    t = per_bank * b + e
-                    cols = slice(P * t, P * (t + 1))
-                    nc.tensor.matmul_mx(
-                        out=z[:, e, :],
-                        lhsT=w1_codes[0][:, cols].bitcast(FP8X4),
-                        lhsT_scale=w1_scale[0][:, cols],
-                        rhs=picked_words[i][h][:, DIRECT_FIRST[h] : DIRECT_FIRST[h] + width].bitcast(FP8X4),
-                        rhs_scale=scale_plane(i, HALF * h + DIRECT_FIRST[h], width),
-                        start=True,
-                        stop=True,
-                    )
-                nc.scalar.activation(direct[i][h][b][:], z[:].rearrange("p e j -> p (e j)"), ACT.Tanh)
+        def encode_direct(i, k, slots, kind="mx"):
+            first, width = GROUPS[k]
+            g = DIRECT_PASS[k]
+            z = bank(kind, [P, len(slots), width])
+            values = held(f"direct{i}{k}{slots[0]}", [P, len(slots), width], F32)
+            words, scale = tokens(i, first, width)
+            for e, t in enumerate(slots):
+                cols = slice(P * t, P * (t + 1))
+                nc.tensor.matmul_mx(
+                    out=z[:, e, :],
+                    lhsT=w1_codes[g][:, cols].bitcast(FP8X4),
+                    lhsT_scale=w1_scale[g][:, cols],
+                    rhs=words,
+                    rhs_scale=scale,
+                    start=True,
+                    stop=True,
+                )
+                direct[i, k, t] = values[:, e, :]
+            nc.scalar.activation(values[:], z[:], ACT.Tanh)
 
         def turned_product(i, g, j, cols, z):
+            words, scale = tokens(i, P * j, P)
             nc.tensor.matmul_mx(
                 out=z,
-                lhsT=picked_words[i][j // TILES][:, P * (j % TILES) : P * (j % TILES + 1)].bitcast(FP8X4),
-                lhsT_scale=scale_plane(i, P * j, P),
+                lhsT=words,
+                lhsT_scale=scale,
                 rhs=w1_codes[g][:, cols].bitcast(FP8X4),
                 rhs_scale=w1_scale[g][:, cols],
                 start=True,
                 stop=True,
             )
 
-        def encode_pair(i, g, pair):
-            if i == SUCCESSORS:
-                both = ring.tile([P, 2, PACK, P], F32, name="turned_successors")[:]
-            elif (g, pair) not in LATE:
-                both = held(f"turned_states{g}{pair}", [P, 2, PACK, P], F32)[:]
-            else:
-                if (g, pair) == LATE[0]:
-                    late["states"] = held("late_states", [P, len(LATE), 2, PACK, P], F32, "w1_raw0")
-                both = late["states"][:, LATE.index((g, pair))]
-            for e in range(2):
-                turned[i][g, 2 * pair + e] = both[:, e]
-            for q in range(2):
-                z = bank("mx", [P, 2, PASS // 2])
+        def encode_piece(i, g, pair, q):
+            if q == 0:
+                late[i, g, pair] = held(f"pair{i}{g}{pair}", [P, 2, PACK, P], F32)
                 for e in range(2):
-                    turned_product(i, g, 2 * pair + e, slice(PASS // 2 * q, PASS // 2 * (q + 1)), z[:, e, :])
-                if g == 1:
-                    dst, src = both[:, :, :, P // 2 * q : P // 2 * (q + 1)], z[:].rearrange("p e (t m) -> p e t m", t=PACK)
-                else:
-                    dst, src = both[:, :, 2 * q : 2 * q + 2, :], z[:].rearrange("p e (t m) -> p e t m", t=2)
-                nc.scalar.activation(dst, src, ACT.Tanh, scale=(-1.0 if i == STATES else 1.0))
-
-        def encode_single(j):
-            turned[SUCCESSORS][1, j] = held(f"last_successors{j}", [P, PACK, P], F32)[:]
-            z = bank("mx", [P, PASS])
-            turned_product(SUCCESSORS, 1, j, slice(0, PASS), z[:])
+                    turned[i, g, 2 * pair + e] = late[i, g, pair][:, e]
+            z = bank("mx", [P, 2, PIECE])
+            for e in range(2):
+                turned_product(i, g, 2 * pair + e, slice(PIECE * q, PIECE * (q + 1)), z[:, e, :])
             nc.scalar.activation(
-                turned[SUCCESSORS][1, j].rearrange("p t (q m) -> p q t m", q=2),
-                z[:].rearrange("p (q t m) -> p q t m", q=2, t=PACK),
+                late[i, g, pair][:, :, 2 * q : 2 * q + 2, :],
+                z[:].rearrange("p e (t m) -> p e t m", t=2),
                 ACT.Tanh,
+                scale=(-1.0 if i == STATES else 1.0),
             )
 
-        def gain_states(h):
-            if h == 0:
-                both = held("gained", [P, PACK * sum(WIDTH)], F32, "w1_bf1")
-                for k in range(2):
-                    first = PACK * WIDTH[0] * k
-                    gained[k] = [both[:, first + WIDTH[k] * t : first + WIDTH[k] * (t + 1)] for t in range(PACK)]
-            for t in range(PACK):
-                nc.vector.tensor_scalar(gained[h][t], direct_slot(STATES, h, t), gains[0][:, 0, t : t + 1], None, ALU.mult)
+        def encode_pair(i, g, pair):
+            for q in range(2):
+                encode_piece(i, g, pair, q)
 
-        def change_direct(h, slots):
+        def encode_tile(i, g, j):
+            turned[i, g, j] = held(f"turned{i}{g}{j}", [P, PACK, P], F32)[:]
+            z = bank("mx", [P, PASS])
+            turned_product(i, g, j, slice(0, PASS), z[:])
+            nc.scalar.activation(turned[i, g, j].rearrange("p t m -> p (t m)"), z[:], ACT.Tanh)
+
+        def gain_states(k, slots):
+            for t in slots:
+                gained[k, t] = held(f"gained{k}{t}", [P, GROUPS[k][1]], F32)[:]
+                column = gains[:, DIRECT_PASS[k], t : t + 1]
+                nc.vector.tensor_scalar(gained[k, t], direct[STATES, k, t], column, None, ALU.mult)
+
+        def gain_states_on_gpsimd(k, slots, on):
+            products = held("gained_late", [P, len(slots), GROUPS[k][1]], F32, on)
+            for e, t in enumerate(slots):
+                gained[k, t] = products[:, e, :]
+                column = gains[:, DIRECT_PASS[k], t : t + 1]
+                nc.gpsimd.tensor_scalar(gained[k, t], direct[STATES, k, t], column, 0.0, ALU.mult, ALU.add)
+
+        def change_direct(k, slots):
+            if k not in h_slots:
+                h_slots[k] = held("h_slots_front", [P, PACK, HALF], BF16, "w1_raw0")
             for t in slots:
                 nc.vector.scalar_tensor_tensor(
-                    h_slots[h][:, t, :],
-                    direct_slot(SUCCESSORS, h, t),
-                    gains[0][:, 0, t : t + 1],
-                    gained[h][t],
+                    h_slots[k][:, t, :],
+                    direct[SUCCESSORS, k, t],
+                    gains[:, DIRECT_PASS[k], t : t + 1],
+                    gained[k, t],
                     ALU.mult,
                     ALU.subtract,
                 )
 
-        def interleave(h, first, width):
-            cols = slice(first, first + width)
+        def interleave(k):
             nc.vector.tensor_copy(
-                h_bf[0][h][:, cols, :].rearrange("p (c e) t -> p c t e", e=4),
-                h_slots[h][:, :, cols].rearrange("p t (c e) -> p c t e", e=4),
+                h_bf[DIRECT_PASS[k]][k][:].rearrange("p (c e) t -> p c t e", e=4),
+                h_slots[k][:].rearrange("p t (c e) -> p c t e", e=4),
             )
 
-        def interleave_on_scalar(h):
-            late["quarter"] = held("late_quarter", [P, QUARTER, PACK], BF16, "picked_words11")
+        def interleave_on_scalar(k):
+            h_bf[LATE][k] = held("late_quarter", [P, QUARTER, PACK], BF16, "picked_words11")
             nc.scalar.copy(
-                late["quarter"][:].rearrange("p (c e) t -> p c t e", e=4),
-                h_slots[h][:].rearrange("p t (c e) -> p c t e", e=4),
+                h_bf[LATE][k][:].rearrange("p (c e) t -> p c t e", e=4),
+                h_slots[k][:].rearrange("p t (c e) -> p c t e", e=4),
             )
 
-        def turn(i, g, j):
+        def turn(i, g, j, kind="turn"):
             first = (g, j) not in difference
             if first:
-                difference[g, j] = bank("turn", [P, PACK, P])
+                difference[g, j] = bank(kind, [P, PACK, P])
             for t in range(PACK):
                 nc.tensor.matmul(
                     difference[g, j][:, PACK - 1 - t, :],
-                    turned[i][g, j][:, PACK - 1 - t, :],
+                    turned[i, g, j][:, PACK - 1 - t, :],
                     ident[:],
                     start=(first and t == 0),
                     stop=(not first and t == PACK - 1),
@@ -263,133 +246,139 @@ def tile_list_replay_inverse_dynamics_kernel(
                 )
 
         def change_turned(g, j):
-            cols = slice(P * (j % TILES), P * (j % TILES + 1))
+            k = max(FRONT, j // 2 - 1)
+            first = P * j - GROUPS[k][0]
             nc.vector.tensor_tensor(
-                h_bf[g][j // TILES][:, cols, :],
+                h_bf[g][k][:, first : first + P, :],
                 difference[g, j][:].rearrange("p t j -> p j t"),
-                gains[g][:].to_broadcast([P, P, PACK]),
+                gains[:, g : g + 1, :].to_broadcast([P, P, PACK]),
                 ALU.mult,
             )
 
-        def logit_products(h, first, width, rows=(0, 1)):
+        def logits(k, kind, order, rows=(0, 1)):
+            width = GROUPS[k][1]
             step = HALF if width == HALF else P
             for c in rows:
-                acc = bank("turn" if first else "mx", [P, width])
-                sums[h, first, c] = acc
-                for n0 in range(0, width, step):
-                    cols = slice(first + n0, first + n0 + step)
-                    for g in (DIRECT, TURNED):
+                acc = bank(kind, [P, width])
+                sums[k, 0, c] = acc
+                for first in range(0, width, step):
+                    cols = slice(first, first + step)
+                    for n, g in enumerate(order):
                         nc.tensor.matmul_mx(
-                            out=acc[:, n0 : n0 + step],
-                            lhsT=w4["codes"][:, g, P // 2 * c : P // 2 * (c + 1)].bitcast(U8).bitcast(FP4X4),
-                            lhsT_scale=w4["scale"][:, g, P // 4 * c : P // 4 * (c + 1)].bitcast(U8),
-                            rhs=h_codes[g][h][:, cols].bitcast(FP8X4),
-                            rhs_scale=h_scale[g][h][:, cols],
-                            start=(g == DIRECT),
-                            stop=(g == TURNED),
+                            out=acc[:, cols],
+                            lhsT=late["w4_codes"][:, g, P // 2 * c : P // 2 * (c + 1)].bitcast(U8).bitcast(FP4X4),
+                            lhsT_scale=late["w4_scale"][:, g, P // 4 * c : P // 4 * (c + 1)].bitcast(U8),
+                            rhs=h_codes[g][k][:, cols].bitcast(FP8X4),
+                            rhs_scale=h_scale[g][k][:, cols],
+                            start=(n == 0),
+                            stop=(n == 1),
                         )
 
-        def store_logits(h, first, width, shared):
-            tokens = slice(HALF * h + first, HALF * h + first + width)
+        def store(k, shared, first=0, width=None):
+            width = width or GROUPS[k][1]
+            where = slice(GROUPS[k][0] + first, GROUPS[k][0] + first + width)
             for c in range(2):
-                result = held(f"result{h}_{first}_{c}", [P, width], F32)
-                acc = sums[h, first, c]
+                result = held(f"result{k}_{first}_{c}", [P, width], F32)
+                acc = sums[k, first, c]
                 if shared and c == 1:
                     nc.vector.tensor_scalar(result[:], acc[:], late["biases"][:, c : c + 1], None, ALU.add)
                 else:
                     nc.scalar.activation(result[:], acc[:], ACT.Identity, bias=late["biases"][:, c : c + 1])
-                nc.sync.dma_start(out_rows[:, c, tokens], result[:])
+                nc.sync.dma_start(out_rows[:, c, where], result[:])
 
         nc.vector.memset(staged_scales[STATES][0 : STAGE_ROWS[STATES].start, :], 0)
         nc.vector.memset(staged_scales[SUCCESSORS][:], 0)
         nc.sync.dma_start(lists[STATES][:], offs)
         load_scales(STATES, tab_scales)
         nc.sync.dma_start(lists[SUCCESSORS][:], offs2)
-        load_w1(DIRECT)
+        load_w1(EARLY)
         load_scales(SUCCESSORS, tab2_scales)
         load_words(STATES, tab_words)
-        load_gain(DIRECT, nc.gpsimd)
+        nc.gpsimd.dma_start(gains[:], gain.rearrange("(g p t) -> p g t", g=2, t=PACK))
         make_identity(nc, ident[:])
 
         gather_scales(STATES)
         place_scales(STATES)
-        load_w1(TURNED, on="staged_scales0")
+        load_words(SUCCESSORS, tab2_words, on="staged_scales0")
         for u in range(2):
-            nc.scalar.activation(*cast_views(DIRECT, u), ACT.Copy)
-        load_words(SUCCESSORS, tab2_words, on="w1_raw0")
+            nc.scalar.activation(*cast_views(EARLY, u), ACT.Copy)
         gather_scales(SUCCESSORS)
-        quantize_w1(DIRECT)
-        place_scales(SUCCESSORS, on="w1_bf0")
-        for h in range(2):
-            gather_words(STATES, h)
-            encode_direct(STATES, h, range(WIDTH[h] // P))
         for u in range(2):
-            cast_turned(u)
-        quantize_w1(TURNED)
-        load_gain(TURNED, nc.sync, on="picked_rows0")
-        load_w4()
-        load_bias(on="table_words0")
-        gain_states(0)
-        gain_states(1)
-        for g, pair in ((1, 0), (1, 1), (0, 2)):
-            encode_pair(STATES, g, pair)
+            quantize_w1(EARLY, u)
+        place_scales(SUCCESSORS, on="w1_bf01")
+        load_w1(LATE, on="w1_raw0")
+        gather_words(STATES, 0)
+        for t in range(PACK):
+            encode_direct(STATES, FRONT, [t])
+        gather_words(STATES, 1)
+        gain_states(FRONT, [0, 1])
+        gain_states_on_gpsimd(FRONT, [2, 3], "direct001")
+        for pair in (2, 3):
+            encode_pair(STATES, EARLY, pair)
         gather_words(SUCCESSORS, 0)
         gather_words(SUCCESSORS, 1)
-        for j in range(TILES):
-            turn(STATES, 1, j)
+        load_rest()
 
-        encode_direct(SUCCESSORS, 0, range(PACK))
-        change_direct(0, range(PACK))
-        encode_pair(SUCCESSORS, 1, 0)
-        encode_pair(SUCCESSORS, 1, 1)
-        interleave(0, 0, HALF)
+        for t in range(PACK):
+            encode_direct(SUCCESSORS, FRONT, [t], "turn")
+        for pair in (2, 3):
+            encode_pair(SUCCESSORS, EARLY, pair)
+        for j in range(4, 8):
+            turn(STATES, EARLY, j)
+        for u in range(2):
+            nc.vector.tensor_copy(*cast_views(LATE, u))
+        for u in range(2):
+            change_direct(FRONT, [u])
+            quantize_w1(LATE, u)
+        change_direct(FRONT, [2, 3])
+        for j in (4, 5):
+            turn(SUCCESSORS, EARLY, j)
+        encode_pair(STATES, LATE, 0)
+        for j in (6, 7):
+            turn(SUCCESSORS, EARLY, j)
+        encode_pair(SUCCESSORS, LATE, 0)
+        change_turned(EARLY, 4)
+        change_turned(EARLY, 5)
+        interleave(FRONT)
+        encode_pair(STATES, LATE, 1)
+        change_turned(EARLY, 6)
+        change_turned(EARLY, 7)
+        for i in range(2):
+            for j in (0, 1):
+                turn(i, LATE, j)
+        encode_pair(SUCCESSORS, LATE, 1)
+        for k in range(3):
+            quantize_h(EARLY, k)
+        for u in range(2):
+            encode_direct(STATES, BACK, [2 * u, 2 * u + 1])
+        for i in range(2):
+            for j in (2, 3):
+                turn(i, LATE, j)
         for j in (0, 1):
-            turn(SUCCESSORS, 1, j)
-        encode_direct(SUCCESSORS, 1, range(2))
-        for j in (0, 1):
-            change_turned(1, j)
+            change_turned(LATE, j)
+        for u in range(2):
+            encode_direct(SUCCESSORS, BACK, [2 * u, 2 * u + 1])
+        gain_states(BACK, range(PACK))
+        change_direct(BACK, range(PACK))
+        encode_pair(STATES, LATE, 2)
         for j in (2, 3):
-            turn(SUCCESSORS, 1, j)
-        for j in (2, 3):
-            change_turned(1, j)
-        encode_pair(SUCCESSORS, 0, 2)
+            change_turned(LATE, j)
         for j in (4, 5):
-            turn(STATES, 0, j)
-        change_direct(1, [0])
-        quantize_h(1, 0, 0, HALF)
-
-        change_direct(1, [1, 2, 3])
-        quantize_h(0, 0, 0, HALF)
-        encode_pair(STATES, 1, 2)
-        encode_pair(SUCCESSORS, 1, 2)
-        for j in (4, 5):
-            turn(SUCCESSORS, 0, j)
-        for j in (4, 5):
-            change_turned(0, j)
-        encode_pair(STATES, 1, 3)
-        for j in (4, 5):
-            turn(STATES, 1, j)
-        for j in (6, 7):
-            encode_single(j)
-        interleave_on_scalar(1)
-        for j in (4, 5):
-            turn(SUCCESSORS, 1, j)
-        logit_products(0, 0, HALF, rows=(0,))
-        for j in (6, 7):
-            turn(STATES, 1, j)
-        for j in (6, 7):
-            turn(SUCCESSORS, 1, j)
-        logit_products(0, 0, HALF, rows=(1,))
-        store_logits(0, 0, HALF, shared=False)
-        change_turned(1, 4)
-        quantize_h(0, 1, 0, QUARTER)
-        change_turned(1, 5)
-        quantize_h(1, 1, 0, QUARTER)
-        change_turned(1, 6)
-        change_turned(1, 7)
-        quantize(h_codes[0][1][:, QUARTER:HALF], h_scale[0][1][:, QUARTER:HALF], late["quarter"][:])
-        quantize_h(1, 1, QUARTER, P)
-        quantize_h(1, 1, QUARTER + P, P)
-        for first in (0, QUARTER):
-            logit_products(1, first, QUARTER)
-            store_logits(1, first, QUARTER, shared=(first > 0))
+            encode_tile(SUCCESSORS, LATE, j)
+        quantize_h(LATE, FRONT)
+        logits(FRONT, "mx", (EARLY, LATE), rows=(0,))
+        interleave_on_scalar(BACK)
+        for i in range(2):
+            for j in (4, 5):
+                turn(i, LATE, j)
+        logits(FRONT, "mx", (EARLY, LATE), rows=(1,))
+        store(FRONT, shared=False)
+        change_turned(LATE, 4)
+        change_turned(LATE, 5)
+        quantize_h(LATE, MIDDLE, 0, P)
+        quantize_h(LATE, BACK)
+        quantize_h(LATE, MIDDLE, P, P)
+        logits(BACK, "mx", (EARLY, LATE))
+        store(BACK, shared=False)
+        logits(MIDDLE, "turn", (EARLY, LATE))
+        store(MIDDLE, shared=True)

@@ -199,7 +199,7 @@ def tile_list_replay_inverse_dynamics_kernel(
                 nc.vector.tensor_scalar(gained[k, t], direct[STATES, k, t], column, None, ALU.mult)
 
         def gain_states_on_gpsimd(k, slots, on):
-            products = held("gained_late", [P, len(slots), GROUPS[k][1]], F32, on)
+            products = held(f"gained_late{k}", [P, len(slots), GROUPS[k][1]], F32, on)
             for e, t in enumerate(slots):
                 gained[k, t] = products[:, e, :]
                 column = gains[:, DIRECT_PASS[k], t : t + 1]
@@ -358,11 +358,11 @@ def tile_list_replay_inverse_dynamics_kernel(
             change_turned(LATE, j)
         for u in range(2):
             encode_direct(SUCCESSORS, BACK, [2 * u, 2 * u + 1])
-        gain_states(BACK, range(PACK))
-        change_direct(BACK, range(PACK))
+        gain_states_on_gpsimd(BACK, range(PACK), "h_bf02")
         encode_pair(STATES, LATE, 2)
         for j in (2, 3):
             change_turned(LATE, j)
+        change_direct(BACK, range(PACK))
         for j in (4, 5):
             encode_tile(SUCCESSORS, LATE, j)
         quantize_h(LATE, FRONT)

from contextlib import ExitStack

import concourse.mybir as mybir
from concourse.masks import make_identity

K, H, N, T, S = 512, 1024, 256, 4096, 1024
FLOPS = 2 * (2 * K * H * S) + 2 * H * N * S

F32 = mybir.dt.float32
BF16 = mybir.dt.bfloat16
I32 = mybir.dt.int32
U32 = mybir.dt.uint32
U16 = mybir.dt.uint16
U8 = mybir.dt.uint8
FP8X4 = mybir.dt.float8_e4m3fn_x4
FP4X4 = mybir.dt.float4_e2m1fn_x4
ACT = mybir.ActivationFunctionType
ALU = mybir.AluOpType

P = 128
PACK = 4
PASS = P * PACK
PIECE = PASS // 2
HALF = S // 2
QUARTER = S // 4
TILES = HALF // P
STRIPE = 16
QUADRANT = 32
SCALE_ROWS = 4
STATES, SUCCESSORS = 0, 1
EARLY, LATE = 0, 1
STAGE_ROWS = (slice(112, 128), slice(32, 96, 4))
SCALE_START = (0, 4)
BANKS = 4
GROUPS = ((0, HALF), (HALF, QUARTER), (HALF + QUARTER, QUARTER))
FRONT, MIDDLE, BACK = 0, 1, 2
DIRECT_PASS = {FRONT: EARLY, BACK: LATE}


def tile_list_replay_inverse_dynamics_kernel(
    tc, tab_words, tab_scales, tab2_words, tab2_scales, offs, offs2, w1, gain, w4_words, w4_scales, bias, out
):
    nc = tc.nc
    with ExitStack() as ctx:
        keep = ctx.enter_context(tc.tile_pool(name="keep", bufs=1))
        psum = ctx.enter_context(tc.psum_pool(name="psum", bufs=1))
        taken = {"mx": 0, "turn": 0}

        def bank(kind, shape):
            taken[kind] = taken[kind] + 1
            return psum.tile(shape, F32, name=f"{kind}{taken[kind]}", tag=f"{kind}_bank{taken[kind] % BANKS}")

        def held(name, shape, dtype, on=None):
            return keep.tile(shape, dtype, name=name, tag=on or name, align_bytes=64)

        lists = [keep.tile([P, S // STRIPE], U16, name=f"list{i}") for i in range(2)]
        staged_scales = [held(f"staged_scales{i}", [P, T // 4], I32) for i in range(2)]
        picked_rows = [held(f"picked_rows{i}", [P, S], U8) for i in range(2)]
        picked_scales = {}
        gains = held("gains", [P, 2, PACK], F32)
        ident = held("ident", [P, P], F32)
        table_words, raw, late = {}, {}, {}
        w1_rows = w1.rearrange("(p i) c -> p i c", i=PACK)

        def load_words(i, src, on=None):
            table_words[i] = held(f"table_words{i}", [P, T], I32, on)
            nc.sync.dma_start(table_words[i][:], src[0].rearrange("p t i -> p (t i)").bitcast(I32))

        def load_w1(g, on=None):
            raw[g] = held(f"w1_raw{g}", [P, PACK, PASS], F32, on)
            nc.sync.dma_start(raw[g][:], w1_rows[:, :, PASS * g : PASS * (g + 1)])

        def load_scales(i, src):
            nc.sync.dma_start(staged_scales[i][STAGE_ROWS[i], :], src[0].bitcast(I32))

        def gather_scales(i):
            nc.vector.tensor_copy(picked_rows[i][:], staged_scales[i][:].bitcast(U8).indirect(lists[i][:]))

        def place_scales(i, on=None):
            picked_scales[i] = held(f"picked_scales{i}", [P, S // 4], I32, on)
            nc.vector.memset(picked_scales[i][:], 0)
            rows = STAGE_ROWS[i]
            step = rows.step or 1
            for r in range(SCALE_ROWS):
                nc.sync.dma_start(
                    picked_scales[i][SCALE_START[i] + r : P : QUADRANT, :],
                    picked_rows[i][rows.start + step * r : rows.stop : step * SCALE_ROWS, :].bitcast(I32),
                )

        def load_rest():
            late["w4_scale"] = held("w4_scale", [P, 2, N // 4], I32, "picked_rows1")
            nc.gpsimd.memset(late["w4_scale"][:], 0)
            late["w4_codes"] = held("w4_codes", [P, 2, N // 2], I32, "staged_scales0")
            nc.sync.dma_start(late["w4_codes"][:], w4_words.bitcast(I32).rearrange("g p c -> p g c"))
            for r in range(SCALE_ROWS):
                nc.sync.dma_start(
                    late["w4_scale"][r:P:QUADRANT, :, :],
                    w4_scales.bitcast(I32)[:, r::SCALE_ROWS, :].rearrange("g q c -> q g c"),
                )
            late["biases"] = held("biases", [P, 2], F32, "table_words0")
            with nc.allow_non_contiguous_dma(reason="one bias for each partition"):
                nc.sync.dma_start(late["biases"][:], bias.rearrange("(c p) -> p c", p=P))

        w1_bf = [[held(f"w1_bf{g}{u}", [P, PIECE, PACK], BF16) for u in range(2)] for g in range(2)]
        w1_codes = [held(f"w1_codes{g}", [P, PASS], U32) for g in range(2)]
        w1_scale = [held(f"w1_scale{g}", [P, PASS], U8) for g in range(2)]
        picked_words = [[held(f"picked_words{i}{h}", [P, HALF], U32) for h in range(2)] for i in range(2)]
        direct, gained, turned, difference, sums = {}, {}, {}, {}, {}
        h_slots = {BACK: held("h_slots_back", [P, PACK, QUARTER], BF16)}
        h_bf = [[held(f"h_bf{g}{k}", [P, GROUPS[k][1], PACK], BF16) for k in range(3 - g)] + [None] * g for g in range(2)]
        h_codes = [[held(f"h_codes{g}{k}", [P, GROUPS[k][1]], U32) for k in range(3)] for g in range(2)]
        h_scale = [[held(f"h_scale{g}{k}", [P, GROUPS[k][1]], U8) for k in range(3)] for g in range(2)]
        out_rows = out.rearrange("(c p) j -> p c j", p=P)

        def tokens(i, first, count):
            words = picked_words[i][first // HALF][:, first % HALF : first % HALF + count].bitcast(FP8X4)
            return words, picked_scales[i][SCALE_START[i] : P, :].bitcast(U8)[:, first : first + count]

        def gather_words(i, h):
            offsets = lists[i][:, HALF * h // STRIPE : HALF * (h + 1) // STRIPE]
            nc.vector.tensor_copy(picked_words[i][h][:], table_words[i][:].bitcast(U32).indirect(offsets))

        def cast_views(g, u):
            dst = w1_bf[g][u][:].rearrange("p (e m) i -> p m e i", e=2)
            return dst, raw[g][:].rearrange("p i (m u e) -> p u m e i", u=2, e=2)[:, u]

        def quantize(codes, scale, src):
            nc.vector.quantize_mx(out=codes.bitcast(FP8X4), scales=scale, in_=src.rearrange("p c i -> p (c i)"))

        def quantize_w1(g, u):
            cols = slice(PIECE * u, PIECE * (u + 1))
            quantize(w1_codes[g][:, cols], w1_scale[g][:, cols], w1_bf[g][u][:])

        def quantize_h(g, k, first=0, width=None):
            cols = slice(first, first + (width or GROUPS[k][1]))
            quantize(h_codes[g][k][:, cols], h_scale[g][k][:, cols], h_bf[g][k][:, cols, :])

        def encode_direct(i, k, slots, kind="mx"):
            first, width = GROUPS[k]
            g = DIRECT_PASS[k]
            z = bank(kind, [P, len(slots), width])
            values = held(f"direct{i}{k}{slots[0]}", [P, len(slots), width], F32)
            words, scale = tokens(i, first, width)
            for e, t in enumerate(slots):
                cols = slice(P * t, P * (t + 1))
                nc.tensor.matmul_mx(
                    out=z[:, e, :],
                    lhsT=w1_codes[g][:, cols].bitcast(FP8X4),
                    lhsT_scale=w1_scale[g][:, cols],
                    rhs=words,
                    rhs_scale=scale,
                    start=True,
                    stop=True,
                )
                direct[i, k, t] = values[:, e, :]
            nc.scalar.activation(values[:], z[:], ACT.Tanh)

        def turned_product(i, g, j, cols, z):
            words, scale = tokens(i, P * j, P)
            nc.tensor.matmul_mx(
                out=z,
                lhsT=words,
                lhsT_scale=scale,
                rhs=w1_codes[g][:, cols].bitcast(FP8X4),
                rhs_scale=w1_scale[g][:, cols],
                start=True,
                stop=True,
            )

        def encode_piece(i, g, pair, q):
            if q == 0:
                late[i, g, pair] = held(f"pair{i}{g}{pair}", [P, 2, PACK, P], F32)
                for e in range(2):
                    turned[i, g, 2 * pair + e] = late[i, g, pair][:, e]
            z = bank("mx", [P, 2, PIECE])
            for e in range(2):
                turned_product(i, g, 2 * pair + e, slice(PIECE * q, PIECE * (q + 1)), z[:, e, :])
            nc.scalar.activation(
                late[i, g, pair][:, :, 2 * q : 2 * q + 2, :],
                z[:].rearrange("p e (t m) -> p e t m", t=2),
                ACT.Tanh,
                scale=(-1.0 if i == STATES else 1.0),
            )

        def encode_pair(i, g, pair):
            for q in range(2):
                encode_piece(i, g, pair, q)

        def encode_tile(i, g, j):
            turned[i, g, j] = held(f"turned{i}{g}{j}", [P, PACK, P], F32)[:]
            z = bank("mx", [P, PASS])
            turned_product(i, g, j, slice(0, PASS), z[:])
            nc.scalar.activation(turned[i, g, j].rearrange("p t m -> p (t m)"), z[:], ACT.Tanh)

        def gain_states(k, slots):
            for t in slots:
                gained[k, t] = held(f"gained{k}{t}", [P, GROUPS[k][1]], F32)[:]
                column = gains[:, DIRECT_PASS[k], t : t + 1]
                nc.vector.tensor_scalar(gained[k, t], direct[STATES, k, t], column, None, ALU.mult)

        def gain_states_on_gpsimd(k, slots, on):
            products = held(f"gained_late{k}", [P, len(slots), GROUPS[k][1]], F32, on)
            for e, t in enumerate(slots):
                gained[k, t] = products[:, e, :]
                column = gains[:, DIRECT_PASS[k], t : t + 1]
                nc.gpsimd.tensor_scalar(gained[k, t], direct[STATES, k, t], column, 0.0, ALU.mult, ALU.add)

        def change_direct(k, slots):
            if k not in h_slots:
                h_slots[k] = held("h_slots_front", [P, PACK, HALF], BF16, "w1_raw0")
            for t in slots:
                nc.vector.scalar_tensor_tensor(
                    h_slots[k][:, t, :],
                    direct[SUCCESSORS, k, t],
                    gains[:, DIRECT_PASS[k], t : t + 1],
                    gained[k, t],
                    ALU.mult,
                    ALU.subtract,
                )

        def interleave(k):
            nc.vector.tensor_copy(
                h_bf[DIRECT_PASS[k]][k][:].rearrange("p (c e) t -> p c t e", e=4),
                h_slots[k][:].rearrange("p t (c e) -> p c t e", e=4),
            )

        def interleave_on_scalar(k):
            h_bf[LATE][k] = held("late_quarter", [P, QUARTER, PACK], BF16, "picked_words11")
            nc.scalar.copy(
                h_bf[LATE][k][:].rearrange("p (c e) t -> p c t e", e=4),
                h_slots[k][:].rearrange("p t (c e) -> p c t e", e=4),
            )

        def turn(i, g, j, kind="turn"):
            first = (g, j) not in difference
            if first:
                difference[g, j] = bank(kind, [P, PACK, P])
            for t in range(PACK):
                nc.tensor.matmul(
                    difference[g, j][:, PACK - 1 - t, :],
                    turned[i, g, j][:, PACK - 1 - t, :],
                    ident[:],
                    start=(first and t == 0),
                    stop=(not first and t == PACK - 1),
                    is_transpose=True,
                )

        def change_turned(g, j):
            k = max(FRONT, j // 2 - 1)
            first = P * j - GROUPS[k][0]
            nc.vector.tensor_tensor(
                h_bf[g][k][:, first : first + P, :],
                difference[g, j][:].rearrange("p t j -> p j t"),
                gains[:, g : g + 1, :].to_broadcast([P, P, PACK]),
                ALU.mult,
            )

        def logits(k, kind, order, rows=(0, 1)):
            width = GROUPS[k][1]
            step = HALF if width == HALF else P
            for c in rows:
                acc = bank(kind, [P, width])
                sums[k, 0, c] = acc
                for first in range(0, width, step):
                    cols = slice(first, first + step)
                    for n, g in enumerate(order):
                        nc.tensor.matmul_mx(
                            out=acc[:, cols],
                            lhsT=late["w4_codes"][:, g, P // 2 * c : P // 2 * (c + 1)].bitcast(U8).bitcast(FP4X4),
                            lhsT_scale=late["w4_scale"][:, g, P // 4 * c : P // 4 * (c + 1)].bitcast(U8),
                            rhs=h_codes[g][k][:, cols].bitcast(FP8X4),
                            rhs_scale=h_scale[g][k][:, cols],
                            start=(n == 0),
                            stop=(n == 1),
                        )

        def store(k, shared, first=0, width=None):
            width = width or GROUPS[k][1]
            where = slice(GROUPS[k][0] + first, GROUPS[k][0] + first + width)
            for c in range(2):
                result = held(f"result{k}_{first}_{c}", [P, width], F32)
                acc = sums[k, first, c]
                if shared and c == 1:
                    nc.vector.tensor_scalar(result[:], acc[:], late["biases"][:, c : c + 1], None, ALU.add)
                else:
                    nc.scalar.activation(result[:], acc[:], ACT.Identity, bias=late["biases"][:, c : c + 1])
                nc.sync.dma_start(out_rows[:, c, where], result[:])

        nc.vector.memset(staged_scales[STATES][0 : STAGE_ROWS[STATES].start, :], 0)
        nc.vector.memset(staged_scales[SUCCESSORS][:], 0)
        nc.sync.dma_start(lists[STATES][:], offs)
        load_scales(STATES, tab_scales)
        nc.sync.dma_start(lists[SUCCESSORS][:], offs2)
        load_w1(EARLY)
        load_scales(SUCCESSORS, tab2_scales)
        load_words(STATES, tab_words)
        nc.gpsimd.dma_start(gains[:], gain.rearrange("(g p t) -> p g t", g=2, t=PACK))
        make_identity(nc, ident[:])

        gather_scales(STATES)
        place_scales(STATES)
        load_words(SUCCESSORS, tab2_words, on="staged_scales0")
        for u in range(2):
            nc.scalar.activation(*cast_views(EARLY, u), ACT.Copy)
        gather_scales(SUCCESSORS)
        for u in range(2):
            quantize_w1(EARLY, u)
        place_scales(SUCCESSORS, on="w1_bf01")
        load_w1(LATE, on="w1_raw0")
        gather_words(STATES, 0)
        for t in range(PACK):
            encode_direct(STATES, FRONT, [t])
        gather_words(STATES, 1)
        gain_states(FRONT, [0, 1])
        gain_states_on_gpsimd(FRONT, [2, 3], "direct001")
        for pair in (2, 3):
            encode_pair(STATES, EARLY, pair)
        gather_words(SUCCESSORS, 0)
        gather_words(SUCCESSORS, 1)
        load_rest()

        for t in range(PACK):
            encode_direct(SUCCESSORS, FRONT, [t], "turn")
        for pair in (2, 3):
            encode_pair(SUCCESSORS, EARLY, pair)
        for j in range(4, 8):
            turn(STATES, EARLY, j)
        for u in range(2):
            nc.vector.tensor_copy(*cast_views(LATE, u))
        for u in range(2):
            change_direct(FRONT, [u])
            quantize_w1(LATE, u)
        change_direct(FRONT, [2, 3])
        for j in (4, 5):
            turn(SUCCESSORS, EARLY, j)
        encode_pair(STATES, LATE, 0)
        for j in (6, 7):
            turn(SUCCESSORS, EARLY, j)
        encode_pair(SUCCESSORS, LATE, 0)
        change_turned(EARLY, 4)
        change_turned(EARLY, 5)
        interleave(FRONT)
        encode_pair(STATES, LATE, 1)
        change_turned(EARLY, 6)
        change_turned(EARLY, 7)
        for i in range(2):
            for j in (0, 1):
                turn(i, LATE, j)
        encode_pair(SUCCESSORS, LATE, 1)
        for k in range(3):
            quantize_h(EARLY, k)
        for u in range(2):
            encode_direct(STATES, BACK, [2 * u, 2 * u + 1])
        for i in range(2):
            for j in (2, 3):
                turn(i, LATE, j)
        for j in (0, 1):
            change_turned(LATE, j)
        for u in range(2):
            encode_direct(SUCCESSORS, BACK, [2 * u, 2 * u + 1])
        gain_states_on_gpsimd(BACK, range(PACK), "h_bf02")
        encode_pair(STATES, LATE, 2)
        for j in (2, 3):
            change_turned(LATE, j)
        change_direct(BACK, range(PACK))
        for j in (4, 5):
            encode_tile(SUCCESSORS, LATE, j)
        quantize_h(LATE, FRONT)
        logits(FRONT, "mx", (EARLY, LATE), rows=(0,))
        interleave_on_scalar(BACK)
        for i in range(2):
            for j in (4, 5):
                turn(i, LATE, j)
        logits(FRONT, "mx", (EARLY, LATE), rows=(1,))
        store(FRONT, shared=False)
        change_turned(LATE, 4)
        change_turned(LATE, 5)
        quantize_h(LATE, MIDDLE, 0, P)
        quantize_h(LATE, BACK)
        quantize_h(LATE, MIDDLE, P, P)
        logits(BACK, "mx", (EARLY, LATE))
        store(BACK, shared=False)
        logits(MIDDLE, "turn", (EARLY, LATE))
        store(MIDDLE, shared=True)
